import numpy as np, ml_dtypes
CORES = [24,25,26,27,28,29,30,31]
N = 8
import mx_ref
BF = ml_dtypes.bfloat16
def gentries(a):
    return np.ascontiguousarray(a.reshape(8, 16, -1).transpose(0, 2, 1)).reshape(8, -1)
def gtable(e):
    e = np.asarray(e); return np.ascontiguousarray(e.reshape(8, -1, 16).transpose(0, 2, 1)).reshape(128, -1).astype(np.int32)
def gcols(t, e):
    v = np.concatenate([t.reshape(8, 16, -1, 4), np.zeros((8, 16, 1, 4), BF)], axis=2)
    return np.ascontiguousarray(np.stack([v[g][:, e[g]] for g in range(8)])).reshape(128, -1)
def tile(rs):
    return np.stack(rs, axis=2).reshape(128, -1).astype(BF)
def pick(q, e):
    c = np.concatenate([q[0].reshape(128, -1, 4), np.zeros((128, 1, 4), np.uint8)], axis=1); s = np.concatenate([q[1], np.ones((16, 1), np.uint8)], axis=1)
    return (np.ascontiguousarray(c[:, e].reshape(128, -1)), np.ascontiguousarray(s[:, e]))
def join(*qs):
    return (np.concatenate([q[0] for q in qs], axis=1), np.concatenate([q[1] for q in qs], axis=1))
def put(q, e, v):
    c, s = q[0].reshape(128, -1, 4).copy(), q[1].copy(); c[:, e] = v[0].reshape(128, -1, 4); s[:, e] = v[1]
    return (c.reshape(128, -1), s)
def pk(c, s):
    return (np.ascontiguousarray(c), mx_ref.live(s))
def emit(q):
    return q[0], q[1]
def packed(v, rng):
    q = [mx_ref.quantize(np.ascontiguousarray(v[r])) for r in range(N)]
    return np.stack([a for a, b in q]), np.stack([mx_ref.plane(b, rng) for a, b in q])
def values_of_codes():
    e, c = np.zeros((128, 128, 4), np.float32), np.zeros((128, 2, 4), np.uint8)
    e[np.arange(128), np.arange(128), 0] = 1
    c[:127, :, 0] = np.arange(256).reshape(2, 128).T[:127]
    return mx_ref.matmul(mx_ref.quantize(e.reshape(128, 512).astype(BF)), (c.reshape(128, 8), np.full((16, 2), 127, np.uint8))).T.reshape(-1).astype(np.float64)
CODE_VALUE, SCALE_VALUE = values_of_codes(), 2.0 ** (np.arange(256) - 127.0)
def decode(q):
    return (CODE_VALUE[q[0]].reshape(16, 8, -1, 4) * SCALE_VALUE[q[1]][:, None, :, None] + 0.0).reshape(128, -1).astype(np.float32)
def f(rng, *shape):
    return mx_ref.flush((rng.standard_normal(shape, dtype=np.float32) * np.exp2(rng.integers(-2, 3, shape[:-1] + (1,)))).astype(BF))
def wide(rng, *shape, cols=0):
    v = rng.standard_normal(shape, dtype=np.float32) * np.exp2(rng.integers(-12, 13, shape)).astype(np.float32)
    if cols: v *= np.repeat(np.exp2(rng.integers(-cols, cols + 1, shape[:-2] + (1, shape[-1] // 4))) * (rng.random(shape[:-2] + (1, shape[-1] // 4)) > 0.0625), 4, axis=-1).astype(np.float32)
    return mx_ref.flush(v.astype(BF))
C, H, R = 448, 256, 3
def follow(copies, far):
    e = np.tile(np.arange(H + C), (8, 1))
    e[:, H:] -= np.where(copies, far, 0)
    for i in range(C.bit_length()): e = np.take_along_axis(e, e, axis=1)
    return e[:, H:]
def alike(a):
    return np.stack([a] * N)
def trim(v):
    v = v.astype(np.float32)
    v[np.abs(v) < np.float32(2.0 ** -16)] = 0
    return v.astype(BF)
def weights(rng, shut=np.zeros(128, bool)):
    w = trim(f(rng, 128, 2048)).reshape(128, 4, 128, 4)
    w[shut] = 0
    w[:, :, shut] = 0
    c, p = packed(alike(w.reshape(128, 2048)), rng)
    return {"wc": c, "ws": p}
def numbers_of(rng):
    return {"x": trim(f(rng, N, 128, 4 * C)), "u": alike(np.array(f(rng, 128, 512))), "v": np.array(f(rng, N, 128, 512)), "dist": alike(gtable(rng.integers(1, H + 1, (8, C))))}
def first():
    return np.arange(128) % 16 < 8
def heads(d, s, a, b):
    x = d["x"].reshape(N, 8, 16, C, 4)
    x[:, :, :8] = (s * a).astype(np.float32).astype(BF)[:, :, None, :, None]
    u = d["u"].reshape(N, 8, 16, 8, 16, 4)
    u[:, :, :, :, 0] = 0
    for g in range(8): u[:, g, :8, g, 0] = b[g]
    return {**d, "x": x.reshape(N, 128, 4 * C), "u": u.reshape(N, 128, 512)}
def setup_inputs(rng):
    return {**numbers_of(rng), **weights(rng)}
def setup_inputs_deep(rng):
    d = numbers_of(rng)
    k = rng.permutation(8)
    far = rng.integers(1, H + 1, (8, C))
    far[k[:4]] = 1
    far[k[4:6]] = H
    s = rng.permuted(np.tile(np.arange(C) % 2 * 2.0 - 1.0, (N, 8, 1)), axis=2)
    for i in (0, 1, 2, 4, 6): s[:, k[i]] = -1
    s[:, k[1], 0] = 1
    for r in range(N): s[r, k[2], rng.permutation(C)[:3]] = 1
    s[:, k[3]] = (rng.permutation(N) % 2 * 2.0 - 1.0)[:, None]
    d["dist"] = alike(gtable(far))
    return {**heads(d, s, 1.0, [1.0] * 8), **weights(rng, first())}
def setup_inputs_near(rng):
    d = numbers_of(rng)
    s = rng.permuted(np.tile(np.arange(C) % 3 - 1.0, (N, 8, 1)), axis=2)
    k = rng.permutation(8)
    h = int(rng.integers(8))
    d = heads(d, s, np.where(k < 6, 2.0 ** -23, 2.0 ** -30)[:, None], [1.0 if k[g] < 4 else 2.0 ** -25 if k[g] < 6 else 2.0 ** -30 for g in range(8)])
    x = d["x"].reshape(N, 8, 16, C, 4)
    x[:, :, 1:8] = 0
    x[:, :, 0, :, 1:] = 0
    x[:, h, 8:] = 0
    x[:, h, 8, :, 0] = 1
    x[:, h, 9, :, 0] = -1
    u = d["u"].reshape(N, 8, 16, 8, 16, 4)
    for g in range(8):
        if k[g] < 4: u[:, h, 8:10, g, 0, 0] = 1
    shut = first()
    shut[16 * h:16 * h + 16] = True
    return {**d, "x": x.reshape(N, 128, 4 * C), "u": u.reshape(N, 128, 512), **weights(rng, shut)}
def setup_inputs_sums(rng):
    d = numbers_of(rng)
    g = 4 + 2 * int(rng.integers(2))
    blk = np.array([4, 5, 6, 7, 2 * g, 2 * g + 1, 2 * g + 2, 2 * g + 3])
    rest = rng.permutation(np.setdiff1d(np.arange(16), blk))
    x = np.zeros((N, 16, 8, C, 4), np.float32)
    w = np.zeros((128, 4, 128, 4), np.float32)
    u = d["u"].reshape(N, 128, 128, 4)
    u[:, :, ::16] = 0
    r, j = np.arange(N)[:, None], np.arange(C)
    o = np.argsort(rng.random((N, C, 8)), axis=2)
    for h in range(8):
        p, b = h // 4, h % 4
        i = np.take_along_axis(o[:, :, :4], np.argsort(rng.random((N, C, 4)), axis=2), axis=2)
        s = np.take_along_axis(o[:, :, 4:], rng.integers(0, 4, (N, C, 1)), axis=2)
        x[r, blk[i[:, :, 0]], p, j, b] = 1
        x[r, blk[i[:, :, 1]], p, j, b] = -1
        x[r, blk[s[:, :, 0]], p, j, b] = rng.choice([-1.0, 1.0], (N, C)) * 2.0 ** -26
        x[:, rest[h], 0, :, 0] = rng.integers(1, 9, (N, C)) * rng.choice([-1.0, 1.0], (N, C)) * 2.0 ** -26
        u[:, 8 * blk + p, 16 * h, b] = 1
        w[8 * blk + p, 0, 8 * rest[h], b] = 64
    c, q = packed(alike(w.reshape(128, 2048).astype(BF)), rng)
    return {**d, "x": x.reshape(N, 128, 4 * C).astype(BF), "u": u.reshape(N, 128, 512), "wc": c, "ws": q}
def setup_inputs_huge(rng):
    d = numbers_of(rng)
    s = rng.permuted(np.tile(np.arange(C) % 2 * 2.0 - 1.0, (N, 8, 1)), axis=2)
    k = rng.permutation(8)
    s[:, k[0]] = -1
    s[:, k[1]] = 1
    return {**heads(d, s, 2.0 ** 30, [2.0 ** 30] * 8), **weights(rng, first())}
def setup_inputs_spread(rng):
    d = setup_inputs(rng)
    d["x"] = trim(wide(rng, N, 128, 4 * C, cols=6))
    return d
def check_inputs(d):
    b = []
    for k in ("x", "u", "v"):
        a = np.abs(d[k].astype(np.float32))
        if not (np.isfinite(a).all() and ((a == 0) | (a >= 2.0 ** -30) & (a <= 2.0 ** 30)).all()): b.append("a value of " + k)
    for k in ("u", "wc", "dist"):
        if (d[k] != d[k][:1]).any(): b.append(k + " differs between ranks")
    s = [mx_ref.live(p) for p in d["ws"]]
    if any((p != s[0]).any() for p in s): b.append("ws differs between ranks")
    if ((d["wc"] == 127) | (d["wc"] == 255)).any(): b.append("a code of wc")
    if (d["dist"] < 1).any() or (d["dist"] > H).any(): b.append("a number of dist")
    return b
def reference(x, u, v, dist, wc, ws):
    w, qu, far = pk(wc[0], ws[0]), mx_ref.quantize(u[0]), gentries(dist[0])
    now = [x[r] for r in range(N)]
    for t in range(R):
        q = [mx_ref.quantize(now[r]) for r in range(N)]
        full = [decode(q[r]) for r in range(N)]
        roots = []
        for r in range(N):
            e = follow(mx_ref.matmul(qu, q[r])[::16] < 0, far)
            halo = full[r - 1][:, 4 * (C - H):] if r > 0 else np.zeros((128, 4 * H), np.float32)
            z = mx_ref.quantize(gcols(np.concatenate([halo, full[r]], axis=1).astype(BF), e))
            now[r] = tile([full[r][:, b::4] + mx_ref.matmul(pick(w, np.arange(128 * b, 128 * b + 128)), z) * np.float32(0.015625) for b in range(4)])
            roots.append(e - H)
    y, ol = np.zeros((N, 128, C), np.float32), np.zeros((N, 8, C), np.float32)
    oc, osc = np.zeros((N, 128, 4 * C), np.uint8), np.zeros((N, 16, C), np.uint8)
    for r in range(N):
        last = mx_ref.quantize(now[r])
        y[r] = mx_ref.matmul(mx_ref.quantize(v[r]), last)
        ol[r] = roots[r]
        oc[r], osc[r] = emit(last)
    return {"y": y, "ol": ol, "oc": oc, "osc": osc}

@@ -1,0 +1,399 @@
+from concourse.mybir import AluOpType as Op, ActivationFunctionType as Act, dt
+
+F32, B16, I32, U16, U8, X4 = "float32", "bfloat16", "int32", "uint16", "uint8", "float8_e4m3fn_x4"
+C, H, R = 448, 256, 3
+LO = C - H
+HALVES = ((LO, C), (0, LO))
+TINY = 2.0 ** -20
+LEVELS = (4, 16, 64)
+RUN, D = C // 4, 16
+
+SCRATCH = {
+    "z": ("sbuf", [128, 4 * C], B16), "xt": ("sbuf", [128, 4 * C], B16),
+    "zq": ("sbuf", [128, C], X4), "zs": ("sbuf", [128, C], U8),
+    "wq": ("sbuf", [128, 512], X4), "wp": ("sbuf", [128, 512], U8),
+    "ut": ("sbuf", [128, 512], B16), "vt": ("sbuf", [128, 512], B16),
+    "ua": ("sbuf", [128, 128], X4), "uas": ("sbuf", [128, 128], U8),
+    "uq": ("sbuf", [128, 128], X4), "us": ("sbuf", [128, 128], U8),
+    "vq": ("sbuf", [128, 128], X4), "vs": ("sbuf", [128, 128], U8),
+    "et": ("sbuf", [128, 2048], B16), "eq": ("sbuf", [128, 512], X4), "es": ("sbuf", [128, 512], U8),
+    "one": ("sbuf", [128, 128], B16), "idt": ("sbuf", [128, 128], B16),
+    "MN": ("sbuf", [128, H + C], F32), "ff": ("sbuf", [128, C], F32),
+    "ex": ("sbuf", [128, C], F32), "exs": ("sbuf", [128, 512], F32), "exn": ("sbuf", [128, C], F32),
+    "ki": ("sbuf", [128, C], F32), "kd": ("sbuf", [128, C], F32), "kt": ("sbuf", [128, 16], I32), "kb": ("sbuf", [128, 16], I32),
+    "p1": ("sbuf", [128, C], F32), "ph": ("sbuf", [128, H], F32), "idx": ("sbuf", [128, C], F32),
+    "db": ("sbuf", [128, C], I32),
+    "pa": ("sbuf", [128, 2], I32), "pm": ("sbuf", [128, 2], I32), "pm3": ("sbuf", [128, 2], I32), "pm4": ("sbuf", [128, 2], I32),
+    "pf": ("sbuf", [128, 2], F32), "p3": ("sbuf", [128, 2], F32), "pe": ("sbuf", [128, 2], F32), "pc": ("sbuf", [128, 2], F32),
+    "c1": ("sbuf", [128, 28], F32), "ga": ("sbuf", [128, 32], F32), "gn": ("sbuf", [128, 32], F32), "nn": ("sbuf", [128, 32], F32),
+    "ul": ("sbuf", [128, 8], I32), "lu": ("sbuf", [128, 8], U16),
+    "coli": ("sbuf", [128, 2], F32), "cold": ("sbuf", [128, 2], F32),
+    "lc": ("sbuf", [128, 28], U16), "lz": ("sbuf", [128, 28], U16), "L3": ("sbuf", [128, 28], U16),
+    "yt": ("sbuf", [128, C], F32), "olt": ("sbuf", [128, C], F32),
+    "ps": ("psum", [128, 4096], F32),
+}
+for _i in range(3):
+    SCRATCH["U%d" % _i] = ("sbuf", [128, D + C], F32)
+    SCRATCH["X%d" % _i] = ("sbuf", [128, D + C], F32)
+    SCRATCH["L%d" % _i] = ("sbuf", [128, 32], U16)
+    for _n in ("ra", "rb", "ta", "tb", "cc"):
+        SCRATCH["%s%d" % (_n, _i)] = ("sbuf", [128, 32], F32)
+    SCRATCH["ti%d" % _i] = ("sbuf", [128, 32], I32)
+    SCRATCH["hq%d" % _i] = ("sbuf", [128, H], X4)
+    SCRATCH["hs%d" % _i] = ("sbuf", [128, H], U8)
+for _i in range(4):
+    SCRATCH["F%d" % _i] = ("sbuf", [128, H + C], B16)
+    SCRATCH["q%d" % _i] = ("sbuf", [128, C], X4)
+    SCRATCH["s%d" % _i] = ("sbuf", [128, C], U8)
+for _i in range(1, R + 1):
+    SCRATCH["t%d" % _i] = ("sbuf", [128, 4 * C], B16)
+
+SEMAPHORES = ["cv", "cs", "ct", "cp", "sent", "arr0", "arr1", "arr2", "ldxh", "ldxl", "ldu", "ldw", "ldb", "ldv", "out"]
+
+
+def rank_program(g, core, T, topo):
+    rank = T.rank_of(core)
+    if rank is None:
+        return
+    n_ranks = len(T.cores)
+    queue = {"v": g.vector, "s": g.scalar, "t": g.tensor, "p": g, "y": g.sync}
+    total = {s: 0 for s in SEMAPHORES}
+    clock = {q: {} for q in queue}
+    log = {}
+
+    def know(q, tok):
+        sem, n, snap = tok
+        if clock[q].get(sem, 0) >= n:
+            return
+        queue[q].wait_ge(T.sem[sem], n)
+        for s, m in snap.items():
+            clock[q][s] = max(clock[q].get(s, 0), m)
+        clock[q][sem] = n
+
+    def depend(q, outs, ins):
+        need = {}
+        for acc, write in [(a, True) for a in outs] + [(a, False) for a in ins]:
+            name, a, b = acc
+            for (c, d, w, oq, tok) in log.get(name, []):
+                if not (a < d and c < b):
+                    continue
+                if name == "ps":
+                    if oq == q and (q == "t" or not (w or write)):
+                        continue
+                elif not (w or write):
+                    continue
+                old = need.get(tok[0])
+                if old is None or old[1] < tok[1]:
+                    need[tok[0]] = tok
+        for tok in sorted(need.values(), key=lambda t: -len(t[2])):
+            know(q, tok)
+
+    def note(q, outs, ins, tok):
+        for acc, write in [(a, True) for a in outs] + [(a, False) for a in ins]:
+            name, a, b = acc
+            old = log.setdefault(name, [])
+            if write:
+                old[:] = [e for e in old if not (a <= e[0] and e[1] <= b)]
+            old.append((a, b, write, q, tok))
+
+    def emit(q, outs, ins, call):
+        depend(q, outs, ins)
+        sem = "c" + q
+        call(queue[q]).then_inc(T.sem[sem], 1)
+        total[sem] += 1
+        note(q, outs, ins, (sem, total[sem], dict(clock[q])))
+
+    def load(q, out, acc, in_, sem, upto):
+        queue[q].dma_start(out, in_).then_inc(T.sem[sem], 16)
+        total[sem] += 16
+        note(q, [acc], [], (sem, upto, dict(clock[q])))
+
+    def store(q, out, in_, acc):
+        depend(q, [], [acc])
+        queue[q].dma_start(out, in_).then_inc(T.sem["out"], 16)
+        total["out"] += 16
+
+    def copy(q, out, oacc, in_, iacc, scale, bias=0.0):
+        if q == "v":
+            emit("v", [oacc], [iacc], lambda e: e.tensor_scalar(out, in_, scale, None, Op.mult))
+        else:
+            emit("s", [oacc], [iacc], lambda e: e.activation(out, in_, Act.Copy, bias=bias, scale=scale))
+
+    def whole(name):
+        return (name, 0, SCRATCH[name][1][1])
+
+    def affine(out, in_, scale, bias=0.0):
+        copy("s", T[out][:], whole(out), T[in_][:], whole(in_), scale, bias)
+
+    def small(out, in_, s1, s2, *ops):
+        a1 = T[s1][:, 0:1] if isinstance(s1, str) else s1
+        ins = [whole(in_)] + ([whole(s1)] if isinstance(s1, str) else [])
+        emit("v", [whole(out)], ins, lambda e: e.tensor_scalar(T[out][:], T[in_][:], a1, s2, *ops))
+
+    def both(out, a, b, op):
+        emit("v", [whole(out)], [whole(a), whole(b)], lambda e: e.tensor_tensor(T[out][:], T[a][:], T[b][:], op))
+
+    def cast(out, in_):
+        emit("v", [whole(out)], [whole(in_)], lambda e: e.tensor_copy(T[out][:], T[in_][:]))
+
+    def quant(qn, sn, tn, a, b):
+        emit("v", [(qn, a, b), (sn, a, b)], [(tn, 4 * a, 4 * b)],
+             lambda e: e.quantize_mx(T[qn][:, a:b], T[sn][:, a:b], T[tn][:, 4 * a:4 * b]))
+
+    def psum(bank):
+        return ("ps", 512 * bank, 512 * bank + 512)
+
+    def product(bank, st, c0, mv, a, b, start=True, stop=True):
+        n = b - a
+        emit("t", [psum(bank)], [(st[0], c0, c0 + 128), (st[1], c0, c0 + 128), (mv[0], a, b), (mv[1], a, b)],
+             lambda e: e.matmul_mx(T.ps[:, 512 * bank:512 * bank + n], T[st[0]][:, c0:c0 + 128], T[st[1]][:, c0:c0 + 128],
+                                   T[mv[0]][:, a:b], T[mv[1]][:, a:b], start, stop))
+
+    def unpack(b, c, d, bank):
+        n = d - c
+        copy("s", T["F%d" % b][:, c:d], ("F%d" % b, c, d), T.ps[:, 512 * bank:512 * bank + n], psum(bank), 2.0 ** -6)
+
+    def iota(name, pattern, base, mult):
+        if SCRATCH[name][2] == I32:
+            emit("p", [whole(name)], [], lambda e: e.iota(T[name][:], pattern, base, mult))
+        else:
+            emit("p", [whole(name)], [], lambda e: e.iota(T[name][:], pattern, base, mult, allow_small_or_imprecise_dtypes=True))
+
+    def fill(name, a, b, value):
+        emit("v", [(name, a, b)], [], lambda e: e.memset(T[name][:, a:b], value))
+
+    E, W, U, V = ("eq", "es"), ("wq", "wp"), ("uq", "us"), ("vq", "vs")
+
+    load("y", T.xt[:, 4 * LO:4 * C], ("xt", 4 * LO, 4 * C), T.x[:, 4 * LO:4 * C], "ldxh", 16)
+    load("s", T.ut[:], ("ut", 0, 512), T.u[:], "ldu", 16)
+    for i in range(16):
+        load("ys"[i % 2], T.db[i:128:16, :], ("db", 0, C), T.dist[:], "ldb", 256)
+        if i == 0:
+            load("s", T.xt[:, 0:4 * LO], ("xt", 0, 4 * LO), T.x[:, 0:4 * LO], "ldxl", 16)
+    load("y", T.wq[:].bitcast(dt.uint8), ("wq", 0, 512), T.wc[:], "ldw", 32)
+    load("y", T.wp[:], ("wp", 0, 512), T.ws[:], "ldw", 32)
+    load("y", T.vt[:], ("vt", 0, 512), T.v[:], "ldv", 16)
+
+    fill("one", 0, 128, 64.0)
+    iota("pa", [[0, 2]], 0, 1)
+    iota("kt", [[1, 16]], 128, -1)
+    iota("gn", [[0, 4], [16, 8]], 0, 0)
+    iota("c1", [[28, 4], [4, 7]], 0, 0)
+    iota("ul", [[16, 8]], 0, 0)
+    iota("ga", [[0, 4], [-16 * (C - 1), 8]], D - RUN * H, 0)
+    emit("p", [whole("idt")], [whole("one")], lambda e: e.affine_select(T.idt[:], T.one[:], [[-1, 128]], Op.is_equal, 0.0, 0, 1))
+    iota("p1", [[1, 4], [4, RUN]], H, 0)
+    iota("ph", [[1, H]], 0, 0)
+    small("pm", "pa", 15, None, Op.bitwise_and)
+    small("kb", "kt", 15, None, Op.bitwise_and)
+    cast("pf", "pm")
+    emit("v", [("kd", 0, 16)], [whole("kb")], lambda e: e.tensor_scalar(T.kd[:, 0:16], T.kb[:], 1.0, 1.0 - 2.0 ** -10, Op.min, Op.subtract))
+    small("pm3", "pa", 3, None, Op.bitwise_and)
+    small("pm4", "pa", 15, 2, Op.bitwise_and, Op.arith_shift_right)
+    small("p3", "pm3", float(RUN), None, Op.mult)
+    both("pe", "p3", "pm4", Op.add)
+    small("lc", "c1", "pe", None, Op.add)
+    cast("lu", "ul")
+    fill("et", 0, 2048, 0.0)
+    for i in range(3):
+        fill("U%d" % i, 0, D, -1.0)
+        fill("X%d" % i, 0, D, -30000.0)
+    for s in range(4):
+        fill("exs", 128 * s + RUN, 128 * s + 128, 0.0)
+    if rank == 0:
+        for b in range(4):
+            fill("F%d" % b, 0, H, 0.0)
+    for out, in_, col in (("nn", "gn", "pf"),):
+        emit("s", [whole(out)], [whole(in_), whole(col)], lambda e: e.activation(T[out][:], T[in_][:], Act.Identity, bias=T[col][:, 0:1]))
+    for i, k in ((1, 28), (2, 7)):
+        affine("ta%d" % i, "nn", -float(C - 1), float(D - H * k))
+    c = 16
+    while c < C:
+        n = min(c, C - c)
+        copy("s", T.kd[:, c:c + n], ("kd", c, c + n), T.kd[:, 0:n], ("kd", 0, n), 1.0)
+        c += n
+    affine("ki", "kd", 2.0 ** 20)
+    affine("coli", "pf", -1024.0, 15360.0)
+    affine("pc", "pf", -float(C - 1))
+    for i, k in ((1, 28), (2, 7)):
+        small("ti%d" % i, "nn", -(k - 1) / 2.0, 1.0 / k, Op.add, Op.mult)
+        small("tb%d" % i, "ti%d" % i, float((C - 1) * k), None, Op.mult)
+        both("cc%d" % i, "ta%d" % i, "tb%d" % i, Op.add)
+
+    def send(t):
+        if rank + 1 == n_ranks:
+            return
+        dst = T.cores[rank + 1]
+        rid, pid = topo.addr(dst)[:2]
+        depend("p", [], [("q%d" % t, LO, C), ("s%d" % t, LO, C)])
+        for out, in_ in ((T["hq%d" % t][:].bitcast(dt.uint8), T["q%d" % t][:, LO:C].bitcast(dt.uint8)), (T["hs%d" % t][:], T["s%d" % t][:, LO:C])):
+            g.remote_dma(out, in_, T.sem["arr%d" % t], T.sem.sent, pid, rid, topo.mask(core, dst))
+            total["sent"] += len(topo.engines(core, dst))
+
+    def arrives(t):
+        n = len(topo.engines(T.cores[rank - 1], core))
+        for name in ("hq%d" % t, "hs%d" % t):
+            log[name] = [(0, H, True, "far", ("arr%d" % t, 2 * n, {}))]
+
+    quant("q0", "s0", "xt", LO, C)
+    send(0)
+    quant("ua", "uas", "ut", 0, 128)
+    emit("s", [whole("us")], [whole("uas"), whole("lu")], lambda e: e.activation(T.us[:], T.uas[:].indirect(T.lu[:]), Act.Copy))
+    emit("v", [whole("uq")], [whole("ua"), whole("lu")],
+         lambda e: e.tensor_copy(T.uq[:].bitcast(dt.uint32), T.ua[:].bitcast(dt.uint32).indirect(T.lu[:])))
+    quant("q0", "s0", "xt", 0, LO)
+    emit("v", [("X0", D, D + C)], [whole("db"), whole("lc"), whole("p1")],
+         lambda e: e.tensor_tensor(T.X0[:, D:D + C], T.db[:].indirect(T.lc[:]), T.p1[:], Op.subtract))
+    affine("idx", "p1", TINY)
+    emit("s", [whole("cc0")], [whole("ga"), whole("pc")], lambda e: e.activation(T.cc0[:], T.ga[:], Act.Identity, bias=T.pc[:, 0:1]))
+    for b in range(4):
+        copy("s", T.et[:, 512 * b + b:512 * b + 512:4], ("et", 512 * b, 512 * b + 512), T.idt[:], whole("idt"), 1.0)
+    copy("s", T.MN[:, 0:H], ("MN", 0, H), T.ph[:], whole("ph"), TINY)
+    affine("cold", "coli", TINY)
+
+    def row(i):
+        for s in range(4):
+            a = D + RUN * s
+            src = T.X0[:, a:a + RUN] if i is None else T["X%d" % i][:, D + s:D + C:4]
+            emit("v", [("exs", 128 * s, 128 * s + RUN)], [("ki", 0, RUN), ("X%d" % (i or 0), D, D + C)],
+                 lambda e: e.tensor_tensor_scan(T.exs[:, 128 * s:128 * s + RUN], T.ki[:, 0:RUN], src, 0.0, Op.add, Op.max))
+
+    def listing(i, k):
+        emit("v", [whole("ra%d" % i)], [whole("exs"), whole("coli")],
+             lambda e: e.tensor_scalar(T["ra%d" % i][:], T.exs[:, 15:512:16], T.coli[:, 0:1], -float(k), Op.subtract, Op.mult))
+        both("rb%d" % i, "ra%d" % i, "cc%d" % i, Op.add)
+        cast("L%d" % i, "rb%d" % i)
+
+    def merge(kind, i, s):
+        dst = "%s%d" % (kind, i)
+        a = D + RUN * s
+        out, oacc = T[dst][:, a:a + RUN], (dst, a, a + RUN)
+        if i == 0:
+            old, iacc = out, oacc
+        else:
+            src = "%s%d" % (kind, i - 1)
+            old, iacc = T[src][:, D + s:D + C:4], (src, D, D + C)
+        if s > 0:
+            emit("v", [oacc], [(dst, 0, a), ("L%d" % i, 8 * s, 8 * s + 7), iacc],
+                 lambda e: e.tensor_tensor(out, T[dst][:, 0:a].indirect(T["L%d" % i][:, 8 * s:8 * s + 7]), old, Op.max))
+        elif i > 0:
+            emit("v", [oacc], [iacc], lambda e: e.tensor_copy(out, old))
+
+    for t in range(R):
+        q = ("q%d" % t, "s%d" % t)
+        land = ("hq%d" % t, "hs%d" % t)
+        new = "t%d" % (t + 1)
+        if t == 0:
+            for h in range(2):
+                product(h, U, 0, q, HALVES[h][0], HALVES[h][1])
+            row(None)
+            listing(0, RUN)
+        for h in range(2):
+            a, b = HALVES[h]
+            emit("v", [("ff", a, b)], [psum(h)],
+                 lambda e: e.tensor_scalar(T.ff[:, a:b], T.ps[:, 512 * h:512 * h + b - a], 0.0, 2.0 ** -10, Op.is_ge, Op.subtract))
+        for s in range(4):
+            a = RUN * s
+            emit("v", [("U0", D + a, D + a + RUN)], [whole("ff"), whole("idx")],
+                 lambda e: e.tensor_tensor_scan(T.U0[:, D + a:D + a + RUN], T.ff[:, s:C:4], T.idx[:, a:a + RUN], 0.0, Op.add, Op.min))
+        if t == 0:
+            quant("eq", "es", "et", 0, 512)
+        for b in range(4):
+            product(4 + b, E, 128 * b, q, 0, C)
+            unpack(b, H, H + C, 4 + b)
+        for i in range(3):
+            for s in range(4):
+                if t == 0:
+                    merge("X", i, s)
+                merge("U", i, s)
+            if t == 0 and i < 2:
+                row(i)
+                listing(i + 1, RUN // LEVELS[i])
+        if t == 0:
+            for s in range(7):
+                emit("v", [("exn", 64 * s, 64 * s + 64)], [("ki", 0, 64), ("X2", D, D + C)],
+                     lambda e: e.tensor_tensor_scan(T.exn[:, 64 * s:64 * s + 64], T.ki[:, 0:64], T.X2[:, D + s:D + C:7], 0.0, Op.add, Op.max))
+            emit("v", [whole("L3")], [whole("exn"), whole("coli")],
+                 lambda e: e.tensor_scalar(T.L3[:], T.exn[:, 15:C:16], T.coli[:, 0:1], -1.0, Op.subtract, Op.mult))
+        for b in range(4):
+            product(4 + b, E, 128 * b, q, 0, LO, True, False)
+        if rank > 0:
+            arrives(t)
+            for b, bank in enumerate((2, 3, 0, 1)):
+                product(bank, E, 128 * b, land, 0, H)
+                unpack(b, 0, H, bank)
+        for b in range(4):
+            product(b, E, 128 * b, q, LO, C, True, False)
+        for i in range(C // 64):
+            c = H + 64 * i
+            emit("v", [("MN", c, c + 64)], [("MN", 0, c), ("L3", 4 * i, 4 * i + 4), ("U2", D, D + C)],
+                 lambda e: e.tensor_tensor(T.MN[:, c:c + 64], T.MN[:, 0:c].indirect(T.L3[:, 4 * i:4 * i + 4]), T.U2[:, D + i:D + C:7], Op.max))
+
+        def collect(a, b):
+            emit("v", [("ex", a, b)], [("kd", a, b), ("MN", H + a, H + b)],
+                 lambda e: e.tensor_tensor_scan(T.ex[:, a:b], T.kd[:, a:b], T.MN[:, H + a:H + b], 0.0, Op.add, Op.max))
+
+        def listed(a, b):
+            emit("v", [("lz", a // 16, b // 16)], [("ex", a, b), whole("cold")],
+                 lambda e: e.tensor_scalar(T.lz[:, a // 16:b // 16], T.ex[:, a + 15:b:16], T.cold[:, 0:1], 2.0 ** 20, Op.subtract, Op.mult))
+
+        def gather(b, h):
+            a, e1 = HALVES[h]
+            out, src = T.z[:, 4 * a + b:4 * e1:4], T["F%d" % b][:, 0:H + C].indirect(T.lz[:, a // 16:e1 // 16])
+            outs, ins = [("z", 4 * a + b, 4 * a + b + 1)], [whole("F%d" % b), ("lz", a // 16, e1 // 16)]
+            if b < 2:
+                emit("v", outs, ins, lambda e: e.tensor_copy(out, src))
+            else:
+                emit("s", outs, ins, lambda e: e.activation(out, src, Act.Copy))
+
+        collect(LO, C)
+        listed(LO, C)
+        gather(0, 0)
+        collect(0, LO)
+        gather(1, 0)
+        listed(0, LO)
+        for b in (2, 3):
+            gather(b, 0)
+        quant("zq", "zs", "z", LO, C)
+        for h in range(2):
+            if h == 1:
+                for b in range(4):
+                    gather(b, 1)
+                quant("zq", "zs", "z", 0, LO)
+            for b in range(4):
+                product(4 * h + b, W, 128 * b, ("zq", "zs"), HALVES[h][0], HALVES[h][1], False, True)
+
+        def finish(qn, h, b):
+            a, e1 = HALVES[h]
+            bank = 4 * h + b
+            copy(qn, T[new][:, 4 * a + b:4 * e1:4], (new, 4 * a + b, 4 * a + b + 1), T.ps[:, 512 * bank:512 * bank + e1 - a], psum(bank), 2.0 ** -6)
+
+        q = ("q%d" % (t + 1), "s%d" % (t + 1))
+        last = t + 1 == R
+        if last:
+            quant("vq", "vs", "vt", 0, 128)
+        for b in range(4):
+            finish("svsv"[b], 0, b)
+        quant(q[0], q[1], new, LO, C)
+        if last:
+            store("y", T.oc[:, 4 * LO:4 * C], T[q[0]][:, LO:C].bitcast(dt.uint8), (q[0], LO, C))
+        else:
+            send(t + 1)
+        product(0, V if last else U, 0, q, LO, C)
+        for b in range(4):
+            finish("svsv"[b], 1, b)
+        quant(q[0], q[1], new, 0, LO)
+        product(1, V if last else U, 0, q, 0, LO)
+
+    copy("s", T.yt[:, LO:C], ("yt", LO, C), T.ps[:, 0:H], psum(0), 1.0)
+    store("s", T.y[:, LO:C], T.yt[:, LO:C], ("yt", LO, C))
+    copy("v", T.yt[:, 0:LO], ("yt", 0, LO), T.ps[:, 512:512 + LO], psum(1), 1.0)
+    copy("s", T.olt[:], whole("olt"), T.MN[:, H:H + C], ("MN", H, H + C), 2.0 ** 20, -float(H))
+    store("s", T.ol[:], T.olt[0:128:16, :], whole("olt"))
+    store("y", T.oc[:, 0:4 * LO], T[q[0]][:, 0:LO].bitcast(dt.uint8), (q[0], 0, LO))
+    for k in range(4):
+        store("y" if k < 2 else "s", T.osc[4 * k:4 * k + 4, :], T[q[1]][32 * k:32 * k + 4, :], (q[1], 0, C))
+    store("y", T.y[:, 0:LO], T.yt[:, 0:LO], ("yt", 0, LO))
+    for sem in SEMAPHORES:
+        if total[sem]:
+            g.wait_ge(T.sem[sem], total[sem])

@@ -20,14 +20,14 @@ SCRATCH = {
     "one": ("sbuf", [128, 128], B16), "idt": ("sbuf", [128, 128], B16),
     "MN": ("sbuf", [128, H + C], F32), "ff": ("sbuf", [128, C], F32),
     "ex": ("sbuf", [128, C], F32), "exs": ("sbuf", [128, 512], F32), "exn": ("sbuf", [128, C], F32),
-    "ki": ("sbuf", [128, C], F32), "kd": ("sbuf", [128, C], F32), "kt": ("sbuf", [128, 16], I32), "kb": ("sbuf", [128, 16], I32),
+    "ki": ("sbuf", [128, RUN], F32), "kd": ("sbuf", [128, RUN], F32), "kt": ("sbuf", [128, RUN], I32), "kb": ("sbuf", [128, RUN], I32),
     "p1": ("sbuf", [128, C], F32), "ph": ("sbuf", [128, H], F32), "idx": ("sbuf", [128, C], F32),
     "db": ("sbuf", [128, C], I32),
     "pa": ("sbuf", [128, 2], I32), "pm": ("sbuf", [128, 2], I32), "pm3": ("sbuf", [128, 2], I32), "pm4": ("sbuf", [128, 2], I32),
-    "pf": ("sbuf", [128, 2], F32), "p3": ("sbuf", [128, 2], F32), "pe": ("sbuf", [128, 2], F32), "pc": ("sbuf", [128, 2], F32),
-    "c1": ("sbuf", [128, 28], F32), "ga": ("sbuf", [128, 32], F32), "gn": ("sbuf", [128, 32], F32), "nn": ("sbuf", [128, 32], F32),
+    "pf": ("sbuf", [128, 2], F32), "p3": ("sbuf", [128, 2], F32), "pe": ("sbuf", [128, 2], F32),
+    "c1": ("sbuf", [128, 28], F32), "gn": ("sbuf", [128, 32], F32), "nn": ("sbuf", [128, 32], F32),
     "ul": ("sbuf", [128, 8], I32), "lu": ("sbuf", [128, 8], U16),
-    "coli": ("sbuf", [128, 2], F32), "cold": ("sbuf", [128, 2], F32),
+    "coli": ("sbuf", [128, 2], F32), "colm": ("sbuf", [128, 2], F32), "cold": ("sbuf", [128, 2], F32),
     "lc": ("sbuf", [128, 28], U16), "lz": ("sbuf", [128, 28], U16), "L3": ("sbuf", [128, 28], U16),
     "yt": ("sbuf", [128, C], F32), "olt": ("sbuf", [128, C], F32),
     "ps": ("psum", [128, 4096], F32),
@@ -36,7 +36,7 @@ for _i in range(3):
     SCRATCH["U%d" % _i] = ("sbuf", [128, D + C], F32)
     SCRATCH["X%d" % _i] = ("sbuf", [128, D + C], F32)
     SCRATCH["L%d" % _i] = ("sbuf", [128, 32], U16)
-    for _n in ("ra", "rb", "ta", "tb", "cc"):
+    for _n in ("ra", "tb", "td", "te", "cc"):
         SCRATCH["%s%d" % (_n, _i)] = ("sbuf", [128, 32], F32)
     SCRATCH["ti%d" % _i] = ("sbuf", [128, 32], I32)
     SCRATCH["hq%d" % _i] = ("sbuf", [128, H], X4)
@@ -125,6 +125,9 @@ def rank_program(g, core, T, topo):
     def affine(out, in_, scale, bias=0.0):
         copy("s", T[out][:], whole(out), T[in_][:], whole(in_), scale, bias)
 
+    def plus(out, in_, col):
+        emit("s", [whole(out)], [whole(in_), whole(col)], lambda e: e.activation(T[out][:], T[in_][:], Act.Identity, bias=T[col][:, 0:1]))
+
     def small(out, in_, s1, s2, *ops):
         a1 = T[s1][:, 0:1] if isinstance(s1, str) else s1
         ins = [whole(in_)] + ([whole(s1)] if isinstance(s1, str) else [])
@@ -164,61 +167,60 @@ def rank_program(g, core, T, topo):
 
     E, W, U, V = ("eq", "es"), ("wq", "wp"), ("uq", "us"), ("vq", "vs")
 
-    load("y", T.xt[:, 4 * LO:4 * C], ("xt", 4 * LO, 4 * C), T.x[:, 4 * LO:4 * C], "ldxh", 16)
-    load("s", T.ut[:], ("ut", 0, 512), T.u[:], "ldu", 16)
     for i in range(16):
         load("ys"[i % 2], T.db[i:128:16, :], ("db", 0, C), T.dist[:], "ldb", 256)
-        if i == 0:
-            load("s", T.xt[:, 0:4 * LO], ("xt", 0, 4 * LO), T.x[:, 0:4 * LO], "ldxl", 16)
+    load("y", T.xt[:, 4 * LO:4 * C], ("xt", 4 * LO, 4 * C), T.x[:, 4 * LO:4 * C], "ldxh", 16)
+    load("s", T.ut[:], ("ut", 0, 512), T.u[:], "ldu", 16)
+    load("s", T.xt[:, 0:4 * LO], ("xt", 0, 4 * LO), T.x[:, 0:4 * LO], "ldxl", 16)
     load("y", T.wq[:].bitcast(dt.uint8), ("wq", 0, 512), T.wc[:], "ldw", 32)
     load("y", T.wp[:], ("wp", 0, 512), T.ws[:], "ldw", 32)
     load("y", T.vt[:], ("vt", 0, 512), T.v[:], "ldv", 16)
 
     fill("one", 0, 128, 64.0)
-    iota("pa", [[0, 2]], 0, 1)
-    iota("kt", [[1, 16]], 128, -1)
-    iota("gn", [[0, 4], [16, 8]], 0, 0)
-    iota("c1", [[28, 4], [4, 7]], 0, 0)
-    iota("ul", [[16, 8]], 0, 0)
-    iota("ga", [[0, 4], [-16 * (C - 1), 8]], D - RUN * H, 0)
+    fill("et", 0, 2048, 0.0)
     emit("p", [whole("idt")], [whole("one")], lambda e: e.affine_select(T.idt[:], T.one[:], [[-1, 128]], Op.is_equal, 0.0, 0, 1))
+    iota("c1", [[28, 4], [4, 7]], 0, 0)
+    iota("pa", [[0, 2]], 0, 1)
+    iota("kt", [[0, 7], [1, 16]], 128, -1)
+    iota("gn", [[0, 4], [16, 8]], 0, 0)
+    iota("ul", [[16, 8]], 0, 0)
     iota("p1", [[1, 4], [4, RUN]], H, 0)
     iota("ph", [[1, H]], 0, 0)
     small("pm", "pa", 15, None, Op.bitwise_and)
     small("kb", "kt", 15, None, Op.bitwise_and)
     cast("pf", "pm")
-    emit("v", [("kd", 0, 16)], [whole("kb")], lambda e: e.tensor_scalar(T.kd[:, 0:16], T.kb[:], 1.0, 1.0 - 2.0 ** -10, Op.min, Op.subtract))
+    small("kd", "kb", 1.0, 1.0 - 2.0 ** -10, Op.min, Op.subtract)
     small("pm3", "pa", 3, None, Op.bitwise_and)
     small("pm4", "pa", 15, 2, Op.bitwise_and, Op.arith_shift_right)
     small("p3", "pm3", float(RUN), None, Op.mult)
     both("pe", "p3", "pm4", Op.add)
     small("lc", "c1", "pe", None, Op.add)
     cast("lu", "ul")
-    fill("et", 0, 2048, 0.0)
-    for i in range(3):
-        fill("U%d" % i, 0, D, -1.0)
-        fill("X%d" % i, 0, D, -30000.0)
-    for s in range(4):
-        fill("exs", 128 * s + RUN, 128 * s + 128, 0.0)
     if rank == 0:
         for b in range(4):
             fill("F%d" % b, 0, H, 0.0)
-    for out, in_, col in (("nn", "gn", "pf"),):
-        emit("s", [whole(out)], [whole(in_), whole(col)], lambda e: e.activation(T[out][:], T[in_][:], Act.Identity, bias=T[col][:, 0:1]))
-    for i, k in ((1, 28), (2, 7)):
-        affine("ta%d" % i, "nn", -float(C - 1), float(D - H * k))
-    c = 16
-    while c < C:
-        n = min(c, C - c)
-        copy("s", T.kd[:, c:c + n], ("kd", c, c + n), T.kd[:, 0:n], ("kd", 0, n), 1.0)
-        c += n
+
+    def nothing(name, value):
+        copy("s", T[name][:, 0:D], (name, 0, D), T.c1[:, 0:D], whole("c1"), 0.0, value)
+
+    PARTS = ((0, RUN), (1, RUN // 4), (2, RUN // 16))
+
+    def part(i, k):
+        affine("td%d" % i, "nn", (C - 1.0) / k, (k * H - D - 0.25) / k)
+        plus("te%d" % i if i else "cc0", "td%d" % i, "colm")
+
+    plus("nn", "gn", "pf")
+    for b in range(4):
+        copy("s", T.et[:, 512 * b + b:512 * b + 512:4], ("et", 512 * b, 512 * b + 512), T.idt[:], whole("idt"), 1.0)
     affine("ki", "kd", 2.0 ** 20)
-    affine("coli", "pf", -1024.0, 15360.0)
-    affine("pc", "pf", -float(C - 1))
-    for i, k in ((1, 28), (2, 7)):
+    copy("s", T.exs[:, 127:512:128], whole("exs"), T.c1[:, 0:4], whole("c1"), 0.0)
+    affine("colm", "pf", 1024.0, -15360.0)
+    part(0, RUN)
+    nothing("X0", -30000.0)
+    for i, k in PARTS[1:]:
         small("ti%d" % i, "nn", -(k - 1) / 2.0, 1.0 / k, Op.add, Op.mult)
-        small("tb%d" % i, "ti%d" % i, float((C - 1) * k), None, Op.mult)
-        both("cc%d" % i, "ta%d" % i, "tb%d" % i, Op.add)
+        small("tb%d" % i, "ti%d" % i, -(C - 1.0), None, Op.mult)
+    quant("eq", "es", "et", 0, 512)
 
     def send(t):
         if rank + 1 == n_ranks:
@@ -235,22 +237,6 @@ def rank_program(g, core, T, topo):
         for name in ("hq%d" % t, "hs%d" % t):
             log[name] = [(0, H, True, "far", ("arr%d" % t, 2 * n, {}))]
 
-    quant("q0", "s0", "xt", LO, C)
-    send(0)
-    quant("ua", "uas", "ut", 0, 128)
-    emit("s", [whole("us")], [whole("uas"), whole("lu")], lambda e: e.activation(T.us[:], T.uas[:].indirect(T.lu[:]), Act.Copy))
-    emit("v", [whole("uq")], [whole("ua"), whole("lu")],
-         lambda e: e.tensor_copy(T.uq[:].bitcast(dt.uint32), T.ua[:].bitcast(dt.uint32).indirect(T.lu[:])))
-    quant("q0", "s0", "xt", 0, LO)
-    emit("v", [("X0", D, D + C)], [whole("db"), whole("lc"), whole("p1")],
-         lambda e: e.tensor_tensor(T.X0[:, D:D + C], T.db[:].indirect(T.lc[:]), T.p1[:], Op.subtract))
-    affine("idx", "p1", TINY)
-    emit("s", [whole("cc0")], [whole("ga"), whole("pc")], lambda e: e.activation(T.cc0[:], T.ga[:], Act.Identity, bias=T.pc[:, 0:1]))
-    for b in range(4):
-        copy("s", T.et[:, 512 * b + b:512 * b + 512:4], ("et", 512 * b, 512 * b + 512), T.idt[:], whole("idt"), 1.0)
-    copy("s", T.MN[:, 0:H], ("MN", 0, H), T.ph[:], whole("ph"), TINY)
-    affine("cold", "coli", TINY)
-
     def row(i):
         for s in range(4):
             a = D + RUN * s
@@ -258,13 +244,14 @@ def rank_program(g, core, T, topo):
             emit("v", [("exs", 128 * s, 128 * s + RUN)], [("ki", 0, RUN), ("X%d" % (i or 0), D, D + C)],
                  lambda e: e.tensor_tensor_scan(T.exs[:, 128 * s:128 * s + RUN], T.ki[:, 0:RUN], src, 0.0, Op.add, Op.max))
 
-    def listing(i, k):
-        emit("v", [whole("ra%d" % i)], [whole("exs"), whole("coli")],
-             lambda e: e.tensor_scalar(T["ra%d" % i][:], T.exs[:, 15:512:16], T.coli[:, 0:1], -float(k), Op.subtract, Op.mult))
-        both("rb%d" % i, "ra%d" % i, "cc%d" % i, Op.add)
-        cast("L%d" % i, "rb%d" % i)
+    def listing(i, k, between=None):
+        emit("v", [whole("ra%d" % i)], [whole("exs"), whole("cc%d" % i)],
+             lambda e: e.tensor_tensor(T["ra%d" % i][:], T.exs[:, 15:512:16], T["cc%d" % i][:], Op.add))
+        if between:
+            between()
+        small("L%d" % i, "ra%d" % i, -float(k), None, Op.mult)
 
-    def merge(kind, i, s):
+    def merge(kind, i, s, qn="v"):
         dst = "%s%d" % (kind, i)
         a = D + RUN * s
         out, oacc = T[dst][:, a:a + RUN], (dst, a, a + RUN)
@@ -277,17 +264,39 @@ def rank_program(g, core, T, topo):
             emit("v", [oacc], [(dst, 0, a), ("L%d" % i, 8 * s, 8 * s + 7), iacc],
                  lambda e: e.tensor_tensor(out, T[dst][:, 0:a].indirect(T["L%d" % i][:, 8 * s:8 * s + 7]), old, Op.max))
         elif i > 0:
-            emit("v", [oacc], [iacc], lambda e: e.tensor_copy(out, old))
+            copy(qn, out, oacc, old, iacc, 1.0)
+
+    emit("v", [("X0", D, D + C)], [whole("db"), whole("lc"), whole("p1")],
+         lambda e: e.tensor_tensor(T.X0[:, D:D + C], T.db[:].indirect(T.lc[:]), T.p1[:], Op.subtract))
+    row(None)
+    listing(0, RUN)
+    quant("q0", "s0", "xt", LO, C)
+    send(0)
+    quant("ua", "uas", "ut", 0, 128)
+    emit("s", [whole("us")], [whole("uas"), whole("lu")], lambda e: e.activation(T.us[:], T.uas[:].indirect(T.lu[:]), Act.Copy))
+    affine("idx", "p1", TINY)
+    nothing("U0", -1.0)
+    for i, k in PARTS[1:]:
+        part(i, k)
+    for i in (1, 2):
+        nothing("X%d" % i, -30000.0)
+        nothing("U%d" % i, -1.0)
+    copy("s", T.MN[:, 0:H], ("MN", 0, H), T.ph[:], whole("ph"), TINY)
+    affine("coli", "pf", -1024.0, 15360.0)
+    affine("cold", "coli", TINY)
+    emit("v", [whole("uq")], [whole("ua"), whole("lu")],
+         lambda e: e.tensor_copy(T.uq[:].bitcast(dt.uint32), T.ua[:].bitcast(dt.uint32).indirect(T.lu[:])))
+    quant("q0", "s0", "xt", 0, LO)
 
     for t in range(R):
         q = ("q%d" % t, "s%d" % t)
         land = ("hq%d" % t, "hs%d" % t)
         new = "t%d" % (t + 1)
+        last = t + 1 == R
         if t == 0:
             for h in range(2):
                 product(h, U, 0, q, HALVES[h][0], HALVES[h][1])
-            row(None)
-            listing(0, RUN)
+            merge("X", 0, 1)
         for h in range(2):
             a, b = HALVES[h]
             emit("v", [("ff", a, b)], [psum(h)],
@@ -296,20 +305,23 @@ def rank_program(g, core, T, topo):
             a = RUN * s
             emit("v", [("U0", D + a, D + a + RUN)], [whole("ff"), whole("idx")],
                  lambda e: e.tensor_tensor_scan(T.U0[:, D + a:D + a + RUN], T.ff[:, s:C:4], T.idx[:, a:a + RUN], 0.0, Op.add, Op.min))
-        if t == 0:
-            quant("eq", "es", "et", 0, 512)
         for b in range(4):
             product(4 + b, E, 128 * b, q, 0, C)
-            unpack(b, H, H + C, 4 + b)
+            if t > 0:
+                unpack(b, H, H + C, 4 + b)
         for i in range(3):
             for s in range(4):
-                if t == 0:
-                    merge("X", i, s)
-                merge("U", i, s)
+                if t == 0 and (i, s) != (0, 1):
+                    merge("X", i, s, "s")
+                if t > 0 or s < 3 or i == 2:
+                    merge("U", i, s, "v" if t else "s")
             if t == 0 and i < 2:
+                both("cc%d" % (i + 1), "te%d" % (i + 1), "tb%d" % (i + 1), Op.add)
                 row(i)
-                listing(i + 1, RUN // LEVELS[i])
+                listing(i + 1, RUN // LEVELS[i], lambda: merge("U", i, 3))
         if t == 0:
+            for b in range(4):
+                unpack(b, H, H + C, 4 + b)
             for s in range(7):
                 emit("v", [("exn", 64 * s, 64 * s + 64)], [("ki", 0, 64), ("X2", D, D + C)],
                      lambda e: e.tensor_tensor_scan(T.exn[:, 64 * s:64 * s + 64], T.ki[:, 0:64], T.X2[:, D + s:D + C:7], 0.0, Op.add, Op.max))
@@ -324,42 +336,43 @@ def rank_program(g, core, T, topo):
                 unpack(b, 0, H, bank)
         for b in range(4):
             product(b, E, 128 * b, q, LO, C, True, False)
-        for i in range(C // 64):
-            c = H + 64 * i
-            emit("v", [("MN", c, c + 64)], [("MN", 0, c), ("L3", 4 * i, 4 * i + 4), ("U2", D, D + C)],
-                 lambda e: e.tensor_tensor(T.MN[:, c:c + 64], T.MN[:, 0:c].indirect(T.L3[:, 4 * i:4 * i + 4]), T.U2[:, D + i:D + C:7], Op.max))
 
         def collect(a, b):
-            emit("v", [("ex", a, b)], [("kd", a, b), ("MN", H + a, H + b)],
-                 lambda e: e.tensor_tensor_scan(T.ex[:, a:b], T.kd[:, a:b], T.MN[:, H + a:H + b], 0.0, Op.add, Op.max))
+            emit("v", [("ex", a, b)], [("kd", 0, b - a), ("MN", H + a, H + b)],
+                 lambda e: e.tensor_tensor_scan(T.ex[:, a:b], T.kd[:, 0:b - a], T.MN[:, H + a:H + b], 0.0, Op.add, Op.max))
 
         def listed(a, b):
             emit("v", [("lz", a // 16, b // 16)], [("ex", a, b), whole("cold")],
                  lambda e: e.tensor_scalar(T.lz[:, a // 16:b // 16], T.ex[:, a + 15:b:16], T.cold[:, 0:1], 2.0 ** 20, Op.subtract, Op.mult))
 
-        def gather(b, h):
+        def gather(qn, b, h):
             a, e1 = HALVES[h]
             out, src = T.z[:, 4 * a + b:4 * e1:4], T["F%d" % b][:, 0:H + C].indirect(T.lz[:, a // 16:e1 // 16])
             outs, ins = [("z", 4 * a + b, 4 * a + b + 1)], [whole("F%d" % b), ("lz", a // 16, e1 // 16)]
-            if b < 2:
+            if qn == "v":
                 emit("v", outs, ins, lambda e: e.tensor_copy(out, src))
             else:
                 emit("s", outs, ins, lambda e: e.activation(out, src, Act.Copy))
 
-        collect(LO, C)
+        for i in range(C // 64):
+            c = H + 64 * i
+            emit("v", [("MN", c, c + 64)], [("MN", 0, c), ("L3", 4 * i, 4 * i + 4), ("U2", D, D + C)],
+                 lambda e: e.tensor_tensor(T.MN[:, c:c + 64], T.MN[:, 0:c].indirect(T.L3[:, 4 * i:4 * i + 4]), T.U2[:, D + i:D + C:7], Op.max))
+            if i > 0:
+                collect(64 * i - 64, 64 * i)
+            if 64 * i - 64 == LO:
+                listed(0, LO)
+        collect(C - 64, C)
         listed(LO, C)
-        gather(0, 0)
-        collect(0, LO)
-        gather(1, 0)
-        listed(0, LO)
-        for b in (2, 3):
-            gather(b, 0)
+        for b in range(4):
+            gather("vvss"[b], b, 0)
+        if last:
+            quant("vq", "vs", "vt", 0, 128)
         quant("zq", "zs", "z", LO, C)
+        for b in range(4):
+            gather("vvss"[b], b, 1)
+        quant("zq", "zs", "z", 0, LO)
         for h in range(2):
-            if h == 1:
-                for b in range(4):
-                    gather(b, 1)
-                quant("zq", "zs", "z", 0, LO)
             for b in range(4):
                 product(4 * h + b, W, 128 * b, ("zq", "zs"), HALVES[h][0], HALVES[h][1], False, True)
 
@@ -369,9 +382,6 @@ def rank_program(g, core, T, topo):
             copy(qn, T[new][:, 4 * a + b:4 * e1:4], (new, 4 * a + b, 4 * a + b + 1), T.ps[:, 512 * bank:512 * bank + e1 - a], psum(bank), 2.0 ** -6)
 
         q = ("q%d" % (t + 1), "s%d" % (t + 1))
-        last = t + 1 == R
-        if last:
-            quant("vq", "vs", "vt", 0, 128)
         for b in range(4):
             finish("svsv"[b], 0, b)
         quant(q[0], q[1], new, LO, C)

@@ -3,8 +3,13 @@ from concourse.mybir import AluOpType as Op, ActivationFunctionType as Act, dt
 F32, B16, I32, U16, U8, X4 = "float32", "bfloat16", "int32", "uint16", "uint8", "float8_e4m3fn_x4"
 C, H, R = 448, 256, 3
 LO = C - H
-HALVES = ((LO, C), (0, LO))
-TINY = 2.0 ** -20
+SPLIT = 192
+PARTS = ((0, SPLIT), (SPLIT, C))
+HEAD = ("oA2 oB2 U01 U02 oA1 U03 oA0 U1v U1s U11 oA3 U12 oB0 U13 U2s oB1 oB3 h0 h1 h2 U2v h3 U21 e1 U22 e0 U23 E0 E3 E1 E2 "
+        "e2 e3")
+ROUND = ("m0 m1 m2 m3 c0:3 lA m4 m5 m6 gA3s gA1s c3:6 gA2s c6:7 gA0v lB zA gB2v gB3s wA3 wA1 gB0s fA1s wA2 wA0 gB1v zB v "
+         "fA2s wB3 wB1 fB3v wB0 fA0s fA3s wB2 fB1s qA fB0v uA fB2v qB x dAs pA uB dBv pB")
+OWN = (6, 7, 4, 5)
 LEVELS = (4, 16, 64)
 RUN, D = C // 4, 16
 
@@ -16,18 +21,16 @@ SCRATCH = {
     "ua": ("sbuf", [128, 128], X4), "uas": ("sbuf", [128, 128], U8),
     "uq": ("sbuf", [128, 128], X4), "us": ("sbuf", [128, 128], U8),
     "vq": ("sbuf", [128, 128], X4), "vs": ("sbuf", [128, 128], U8),
-    "et": ("sbuf", [128, 2048], B16), "eq": ("sbuf", [128, 512], X4), "es": ("sbuf", [128, 512], U8),
-    "one": ("sbuf", [128, 128], B16), "idt": ("sbuf", [128, 128], B16),
+    "one": ("sbuf", [128, 516], B16), "et": ("sbuf", [128, 516], B16), "eq": ("sbuf", [128, 512], X4), "es": ("sbuf", [128, 512], U8),
     "MN": ("sbuf", [128, H + C], F32), "ff": ("sbuf", [128, C], F32),
-    "ex": ("sbuf", [128, C], F32), "exs": ("sbuf", [128, 512], F32), "exn": ("sbuf", [128, C], F32),
-    "ki": ("sbuf", [128, RUN], F32), "kd": ("sbuf", [128, RUN], F32), "kt": ("sbuf", [128, RUN], I32), "kb": ("sbuf", [128, RUN], I32),
-    "p1": ("sbuf", [128, C], F32), "ph": ("sbuf", [128, H], F32), "idx": ("sbuf", [128, C], F32),
-    "db": ("sbuf", [128, C], I32),
+    "ex": ("sbuf", [128, C], F32), "exs": ("sbuf", [128, 384], F32), "exn": ("sbuf", [128, C], F32),
+    "ki": ("sbuf", [128, H], F32), "kt": ("sbuf", [128, RUN], I32), "kb": ("sbuf", [128, RUN], I32), "kd": ("sbuf", [128, RUN], F32),
+    "p1": ("sbuf", [128, C], F32), "db": ("sbuf", [128, C], I32),
     "pa": ("sbuf", [128, 2], I32), "pm": ("sbuf", [128, 2], I32), "pm3": ("sbuf", [128, 2], I32), "pm4": ("sbuf", [128, 2], I32),
     "pf": ("sbuf", [128, 2], F32), "p3": ("sbuf", [128, 2], F32), "pe": ("sbuf", [128, 2], F32),
-    "c1": ("sbuf", [128, 28], F32), "gn": ("sbuf", [128, 32], F32), "nn": ("sbuf", [128, 32], F32),
+    "c1": ("sbuf", [128, 28], F32), "gn": ("sbuf", [128, 24], F32), "nn": ("sbuf", [128, 24], F32),
     "ul": ("sbuf", [128, 8], I32), "lu": ("sbuf", [128, 8], U16),
-    "coli": ("sbuf", [128, 2], F32), "colm": ("sbuf", [128, 2], F32), "cold": ("sbuf", [128, 2], F32),
+    "coli": ("sbuf", [128, 2], F32), "colm": ("sbuf", [128, 2], F32),
     "lc": ("sbuf", [128, 28], U16), "lz": ("sbuf", [128, 28], U16), "L3": ("sbuf", [128, 28], U16),
     "yt": ("sbuf", [128, C], F32), "olt": ("sbuf", [128, C], F32),
     "ps": ("psum", [128, 4096], F32),
@@ -35,10 +38,10 @@ SCRATCH = {
 for _i in range(3):
     SCRATCH["U%d" % _i] = ("sbuf", [128, D + C], F32)
     SCRATCH["X%d" % _i] = ("sbuf", [128, D + C], F32)
-    SCRATCH["L%d" % _i] = ("sbuf", [128, 32], U16)
+    SCRATCH["L%d" % _i] = ("sbuf", [128, 24], U16)
     for _n in ("ra", "tb", "td", "te", "cc"):
-        SCRATCH["%s%d" % (_n, _i)] = ("sbuf", [128, 32], F32)
-    SCRATCH["ti%d" % _i] = ("sbuf", [128, 32], I32)
+        SCRATCH["%s%d" % (_n, _i)] = ("sbuf", [128, 24], F32)
+    SCRATCH["ti%d" % _i] = ("sbuf", [128, 24], I32)
     SCRATCH["hq%d" % _i] = ("sbuf", [128, H], X4)
     SCRATCH["hs%d" % _i] = ("sbuf", [128, H], U8)
 for _i in range(4):
@@ -48,7 +51,7 @@ for _i in range(4):
 for _i in range(1, R + 1):
     SCRATCH["t%d" % _i] = ("sbuf", [128, 4 * C], B16)
 
-SEMAPHORES = ["cv", "cs", "ct", "cp", "sent", "arr0", "arr1", "arr2", "ldxh", "ldxl", "ldu", "ldw", "ldb", "ldv", "out"]
+SEMAPHORES = ["cv", "cs", "ct", "cp", "sent", "arr0", "arr1", "arr2", "ldxa", "ldxb", "ldu", "ldw", "ldb", "ldv", "out"]
 
 
 def rank_program(g, core, T, topo):
@@ -156,71 +159,68 @@ def rank_program(g, core, T, topo):
         n = d - c
         copy("s", T["F%d" % b][:, c:d], ("F%d" % b, c, d), T.ps[:, 512 * bank:512 * bank + n], psum(bank), 2.0 ** -6)
 
-    def iota(name, pattern, base, mult):
+    def iota(name, pattern, base, mult, b=None):
+        b = b or SCRATCH[name][1][1]
         if SCRATCH[name][2] == I32:
-            emit("p", [whole(name)], [], lambda e: e.iota(T[name][:], pattern, base, mult))
+            emit("p", [(name, 0, b)], [], lambda e: e.iota(T[name][:, 0:b], pattern, base, mult))
         else:
-            emit("p", [whole(name)], [], lambda e: e.iota(T[name][:], pattern, base, mult, allow_small_or_imprecise_dtypes=True))
-
-    def fill(name, a, b, value):
-        emit("v", [(name, a, b)], [], lambda e: e.memset(T[name][:, a:b], value))
+            emit("p", [(name, 0, b)], [], lambda e: e.iota(T[name][:, 0:b], pattern, base, mult, allow_small_or_imprecise_dtypes=True))
 
     E, W, U, V = ("eq", "es"), ("wq", "wp"), ("uq", "us"), ("vq", "vs")
 
     for i in range(16):
         load("ys"[i % 2], T.db[i:128:16, :], ("db", 0, C), T.dist[:], "ldb", 256)
-    load("y", T.xt[:, 4 * LO:4 * C], ("xt", 4 * LO, 4 * C), T.x[:, 4 * LO:4 * C], "ldxh", 16)
+    load("y", T.xt[:, 0:4 * SPLIT], ("xt", 0, 4 * SPLIT), T.x[:, 0:4 * SPLIT], "ldxa", 16)
     load("s", T.ut[:], ("ut", 0, 512), T.u[:], "ldu", 16)
-    load("s", T.xt[:, 0:4 * LO], ("xt", 0, 4 * LO), T.x[:, 0:4 * LO], "ldxl", 16)
+    load("s", T.xt[:, 4 * SPLIT:4 * C], ("xt", 4 * SPLIT, 4 * C), T.x[:, 4 * SPLIT:4 * C], "ldxb", 16)
     load("y", T.wq[:].bitcast(dt.uint8), ("wq", 0, 512), T.wc[:], "ldw", 32)
     load("y", T.wp[:], ("wp", 0, 512), T.ws[:], "ldw", 32)
     load("y", T.vt[:], ("vt", 0, 512), T.v[:], "ldv", 16)
 
-    fill("one", 0, 128, 64.0)
-    fill("et", 0, 2048, 0.0)
-    emit("p", [whole("idt")], [whole("one")], lambda e: e.affine_select(T.idt[:], T.one[:], [[-1, 128]], Op.is_equal, 0.0, 0, 1))
-    iota("c1", [[28, 4], [4, 7]], 0, 0)
     iota("pa", [[0, 2]], 0, 1)
+    iota("c1", [[28, 4], [4, 7]], 0, 0)
+    iota("gn", [[0, 3], [16, 8]], 0, 0)
     iota("kt", [[0, 7], [1, 16]], 128, -1)
-    iota("gn", [[0, 4], [16, 8]], 0, 0)
     iota("ul", [[16, 8]], 0, 0)
     iota("p1", [[1, 4], [4, RUN]], H, 0)
-    iota("ph", [[1, H]], 0, 0)
-    small("pm", "pa", 15, None, Op.bitwise_and)
-    small("kb", "kt", 15, None, Op.bitwise_and)
-    cast("pf", "pm")
-    small("kd", "kb", 1.0, 1.0 - 2.0 ** -10, Op.min, Op.subtract)
+    iota("one", [[0, 516]], 64, 0)
+    emit("p", [whole("et")], [whole("one")], lambda e: e.affine_select(T.et[:], T.one[:], [[-1, 516]], Op.is_equal, 0.0, 3, 4))
+    iota("MN", [[1, H]], 0, 0, H)
     small("pm3", "pa", 3, None, Op.bitwise_and)
     small("pm4", "pa", 15, 2, Op.bitwise_and, Op.arith_shift_right)
+    small("pm", "pa", 15, None, Op.bitwise_and)
     small("p3", "pm3", float(RUN), None, Op.mult)
+    cast("pf", "pm")
     both("pe", "p3", "pm4", Op.add)
     small("lc", "c1", "pe", None, Op.add)
+    small("kb", "kt", 15, None, Op.bitwise_and)
+    small("kd", "kb", 1.0, 1.0 - 2.0 ** -10, Op.min, Op.subtract)
     cast("lu", "ul")
     if rank == 0:
         for b in range(4):
-            fill("F%d" % b, 0, H, 0.0)
+            emit("v", [("F%d" % b, 0, H)], [], lambda e: e.memset(T["F%d" % b][:, 0:H], 0.0))
 
     def nothing(name, value):
         copy("s", T[name][:, 0:D], (name, 0, D), T.c1[:, 0:D], whole("c1"), 0.0, value)
 
-    PARTS = ((0, RUN), (1, RUN // 4), (2, RUN // 16))
+    def keep(a):
+        n = min(RUN, H - a)
+        copy("s", T.ki[:, a:a + n], ("ki", a, a + n), T.kd[:, 0:n], whole("kd"), 2.0 ** 20)
 
-    def part(i, k):
+    COUNTS = ((0, RUN), (1, RUN // 4), (2, RUN // 16))
+    plus("nn", "gn", "pf")
+    affine("colm", "pf", 1024.0, -15360.0)
+    keep(0)
+    copy("s", T.exs[:, 127:384:128], whole("exs"), T.c1[:, 0:3], whole("c1"), 0.0)
+    for i, k in COUNTS:
         affine("td%d" % i, "nn", (C - 1.0) / k, (k * H - D - 0.25) / k)
         plus("te%d" % i if i else "cc0", "td%d" % i, "colm")
-
-    plus("nn", "gn", "pf")
-    for b in range(4):
-        copy("s", T.et[:, 512 * b + b:512 * b + 512:4], ("et", 512 * b, 512 * b + 512), T.idt[:], whole("idt"), 1.0)
-    affine("ki", "kd", 2.0 ** 20)
-    copy("s", T.exs[:, 127:512:128], whole("exs"), T.c1[:, 0:4], whole("c1"), 0.0)
-    affine("colm", "pf", 1024.0, -15360.0)
-    part(0, RUN)
     nothing("X0", -30000.0)
-    for i, k in PARTS[1:]:
+    for i, k in COUNTS[1:]:
         small("ti%d" % i, "nn", -(k - 1) / 2.0, 1.0 / k, Op.add, Op.mult)
         small("tb%d" % i, "ti%d" % i, -(C - 1.0), None, Op.mult)
-    quant("eq", "es", "et", 0, 512)
+    for i, k in COUNTS[1:]:
+        both("cc%d" % i, "te%d" % i, "tb%d" % i, Op.add)
 
     def send(t):
         if rank + 1 == n_ranks:
@@ -238,115 +238,155 @@ def rank_program(g, core, T, topo):
             log[name] = [(0, H, True, "far", ("arr%d" % t, 2 * n, {}))]
 
     def row(i):
-        for s in range(4):
-            a = D + RUN * s
+        for s in range(1, 4):
+            a, c = D + RUN * s, 128 * s - 128
             src = T.X0[:, a:a + RUN] if i is None else T["X%d" % i][:, D + s:D + C:4]
-            emit("v", [("exs", 128 * s, 128 * s + RUN)], [("ki", 0, RUN), ("X%d" % (i or 0), D, D + C)],
-                 lambda e: e.tensor_tensor_scan(T.exs[:, 128 * s:128 * s + RUN], T.ki[:, 0:RUN], src, 0.0, Op.add, Op.max))
+            emit("v", [("exs", c, c + RUN)], [("ki", 0, RUN), ("X%d" % (i or 0), D, D + C)],
+                 lambda e: e.tensor_tensor_scan(T.exs[:, c:c + RUN], T.ki[:, 0:RUN], src, 0.0, Op.add, Op.max))
 
     def listing(i, k, between=None):
         emit("v", [whole("ra%d" % i)], [whole("exs"), whole("cc%d" % i)],
-             lambda e: e.tensor_tensor(T["ra%d" % i][:], T.exs[:, 15:512:16], T["cc%d" % i][:], Op.add))
+             lambda e: e.tensor_tensor(T["ra%d" % i][:], T.exs[:, 15:384:16], T["cc%d" % i][:], Op.add))
         if between:
             between()
         small("L%d" % i, "ra%d" % i, -float(k), None, Op.mult)
 
-    def merge(kind, i, s, qn="v"):
-        dst = "%s%d" % (kind, i)
+    def merge(kind, i, s):
+        dst, src = "%s%d" % (kind, i), "%s%d" % (kind, i - 1)
         a = D + RUN * s
         out, oacc = T[dst][:, a:a + RUN], (dst, a, a + RUN)
         if i == 0:
             old, iacc = out, oacc
         else:
-            src = "%s%d" % (kind, i - 1)
             old, iacc = T[src][:, D + s:D + C:4], (src, D, D + C)
-        if s > 0:
-            emit("v", [oacc], [(dst, 0, a), ("L%d" % i, 8 * s, 8 * s + 7), iacc],
-                 lambda e: e.tensor_tensor(out, T[dst][:, 0:a].indirect(T["L%d" % i][:, 8 * s:8 * s + 7]), old, Op.max))
-        elif i > 0:
-            copy(qn, out, oacc, old, iacc, 1.0)
+        emit("v", [oacc], [(dst, 0, a), whole("L%d" % i), iacc],
+             lambda e: e.tensor_tensor(out, T[dst][:, 0:a].indirect(T["L%d" % i][:, 8 * s - 8:8 * s - 1]), old, Op.max))
+
+    def first(kind, i, qn, r0, r1):
+        dst, src = "%s%d" % (kind, i), "%s%d" % (kind, i - 1)
+        a, b, c, d = D + RUN // 4 * r0, D + RUN // 4 * r1, D + RUN * r0, D + RUN * r1
+        copy(qn, T[dst][:, a:b], (dst, a, b), T[src][:, c:d:4], (src, c, d), 1.0)
+
+    def decide(h, qn):
+        a, b = PARTS[h]
+        in_, bank = T.ps[:, 2048 + 512 * h:2048 + 512 * h + b - a], psum(4 + h)
+        if qn == "v":
+            emit("v", [("ff", a, b)], [bank], lambda e: e.tensor_scalar(T.ff[:, a:b], in_, 0.0, None, Op.is_ge))
+        else:
+            emit("s", [("ff", a, b)], [bank], lambda e: e.activation(T.ff[:, a:b], in_, Act.Sign, bias=2.0 ** -100))
+
+    def places(h):
+        a, b = PARTS[h]
+        for s in range(4):
+            c, d = RUN * s + a // 4, RUN * s + b // 4
+            emit("v", [("U0", D + c, D + d)], [("ff", a, b), ("p1", c, d)],
+                 lambda e: e.tensor_tensor_scan(T.U0[:, D + c:D + d], T.p1[:, c:d], T.ff[:, a + s:b:4], 0.0, Op.max, Op.mult))
 
     emit("v", [("X0", D, D + C)], [whole("db"), whole("lc"), whole("p1")],
          lambda e: e.tensor_tensor(T.X0[:, D:D + C], T.db[:].indirect(T.lc[:]), T.p1[:], Op.subtract))
     row(None)
     listing(0, RUN)
-    quant("q0", "s0", "xt", LO, C)
-    send(0)
     quant("ua", "uas", "ut", 0, 128)
     emit("s", [whole("us")], [whole("uas"), whole("lu")], lambda e: e.activation(T.us[:], T.uas[:].indirect(T.lu[:]), Act.Copy))
-    affine("idx", "p1", TINY)
+    quant("q0", "s0", "xt", 0, SPLIT)
     nothing("U0", -1.0)
-    for i, k in PARTS[1:]:
-        part(i, k)
+    keep(RUN)
     for i in (1, 2):
         nothing("X%d" % i, -30000.0)
         nothing("U%d" % i, -1.0)
-    copy("s", T.MN[:, 0:H], ("MN", 0, H), T.ph[:], whole("ph"), TINY)
     affine("coli", "pf", -1024.0, 15360.0)
-    affine("cold", "coli", TINY)
     emit("v", [whole("uq")], [whole("ua"), whole("lu")],
          lambda e: e.tensor_copy(T.uq[:].bitcast(dt.uint32), T.ua[:].bitcast(dt.uint32).indirect(T.lu[:])))
-    quant("q0", "s0", "xt", 0, LO)
+    keep(2 * RUN)
+    product(4, U, 0, ("q0", "s0"), 0, SPLIT)
+    decide(0, "s")
+    quant("q0", "s0", "xt", SPLIT, C)
+    send(0)
+    product(5, U, 0, ("q0", "s0"), SPLIT, C)
+    merge("X", 0, 1)
+    for b in range(4):
+        c = 128 * b
+        emit("v", [("eq", c, c + 128), ("es", c, c + 128)], [whole("et")],
+             lambda e: e.quantize_mx(T.eq[:, c:c + 128], T.es[:, c:c + 128], T.et[:, 3 - b:515 - b]))
+    places(0)
+    decide(1, "v")
+    places(1)
 
     for t in range(R):
         q = ("q%d" % t, "s%d" % t)
         land = ("hq%d" % t, "hs%d" % t)
         new = "t%d" % (t + 1)
         last = t + 1 == R
+        if rank > 0:
+            arrives(t)
+
+        def head(step):
+            k, h, b = step[0], "AB".find(step[1]), step[2] if step[0] in "oU" else step[1]
+            if k == "U":
+                if b == "s":
+                    first("U", int(step[1]), "s", 0, 3)
+                elif b == "v":
+                    first("U", int(step[1]), "v", 3, 4)
+                else:
+                    merge("U", int(step[1]), int(b))
+                return
+            b = int(b)
+            if k == "o":
+                a, e1 = PARTS[h]
+                bank = b if h else OWN[b]
+                product(bank, E, 128 * b, q, a, e1)
+                unpack(b, H + a, H + e1, bank)
+            elif k == "h" and rank > 0:
+                product(4 + b, E, 128 * b, land, 0, H)
+                unpack(b, 0, H, 4 + b)
+            elif k == "e":
+                product(4 + b, E, 128 * b, q, 0, SPLIT, True, False)
+            elif k == "E":
+                product(b, E, 128 * b, q, SPLIT, C, True, False)
+
         if t == 0:
-            for h in range(2):
-                product(h, U, 0, q, HALVES[h][0], HALVES[h][1])
-            merge("X", 0, 1)
-        for h in range(2):
-            a, b = HALVES[h]
-            emit("v", [("ff", a, b)], [psum(h)],
-                 lambda e: e.tensor_scalar(T.ff[:, a:b], T.ps[:, 512 * h:512 * h + b - a], 0.0, 2.0 ** -10, Op.is_ge, Op.subtract))
-        for s in range(4):
-            a = RUN * s
-            emit("v", [("U0", D + a, D + a + RUN)], [whole("ff"), whole("idx")],
-                 lambda e: e.tensor_tensor_scan(T.U0[:, D + a:D + a + RUN], T.ff[:, s:C:4], T.idx[:, a:a + RUN], 0.0, Op.add, Op.min))
-        for b in range(4):
-            product(4 + b, E, 128 * b, q, 0, C)
-            if t > 0:
-                unpack(b, H, H + C, 4 + b)
-        for i in range(3):
-            for s in range(4):
-                if t == 0 and (i, s) != (0, 1):
-                    merge("X", i, s, "s")
-                if t > 0 or s < 3 or i == 2:
-                    merge("U", i, s, "v" if t else "s")
-            if t == 0 and i < 2:
-                both("cc%d" % (i + 1), "te%d" % (i + 1), "tb%d" % (i + 1), Op.add)
-                row(i)
-                listing(i + 1, RUN // LEVELS[i], lambda: merge("U", i, 3))
-        if t == 0:
-            for b in range(4):
-                unpack(b, H, H + C, 4 + b)
+            for i in range(3):
+                if i > 0:
+                    first("X", i, "s", 0, 4)
+                    first("U", i, "s", 0, 4)
+                for s in range(1, 4):
+                    if (i, s) != (0, 1):
+                        merge("X", i, s)
+                    if s < 3 or i == 2:
+                        merge("U", i, s)
+                if i < 2:
+                    row(i)
+                    listing(i + 1, RUN // LEVELS[i], lambda: merge("U", i, 3))
+                if i > 0:
+                    for b in range(4):
+                        head("o" + " AB"[i] + str(b))
             for s in range(7):
                 emit("v", [("exn", 64 * s, 64 * s + 64)], [("ki", 0, 64), ("X2", D, D + C)],
                      lambda e: e.tensor_tensor_scan(T.exn[:, 64 * s:64 * s + 64], T.ki[:, 0:64], T.X2[:, D + s:D + C:7], 0.0, Op.add, Op.max))
             emit("v", [whole("L3")], [whole("exn"), whole("coli")],
                  lambda e: e.tensor_scalar(T.L3[:], T.exn[:, 15:C:16], T.coli[:, 0:1], -1.0, Op.subtract, Op.mult))
-        for b in range(4):
-            product(4 + b, E, 128 * b, q, 0, LO, True, False)
-        if rank > 0:
-            arrives(t)
-            for b, bank in enumerate((2, 3, 0, 1)):
-                product(bank, E, 128 * b, land, 0, H)
-                unpack(b, 0, H, bank)
-        for b in range(4):
-            product(b, E, 128 * b, q, LO, C, True, False)
+            for k in "heE":
+                for b in range(4):
+                    head(k + str(b))
+        else:
+            for step in HEAD.split():
+                head(step)
+
+        def block(i):
+            c = H + 64 * i
+            emit("v", [("MN", c, c + 64)], [("MN", 0, c), ("L3", 4 * i, 4 * i + 4), ("U2", D, D + C)],
+                 lambda e: e.tensor_tensor(T.MN[:, c:c + 64], T.MN[:, 0:c].indirect(T.L3[:, 4 * i:4 * i + 4]), T.U2[:, D + i:D + C:7], Op.max))
 
         def collect(a, b):
-            emit("v", [("ex", a, b)], [("kd", 0, b - a), ("MN", H + a, H + b)],
-                 lambda e: e.tensor_tensor_scan(T.ex[:, a:b], T.kd[:, 0:b - a], T.MN[:, H + a:H + b], 0.0, Op.add, Op.max))
+            emit("v", [("ex", a, b)], [("ki", 0, b - a), ("MN", H + a, H + b)],
+                 lambda e: e.tensor_tensor_scan(T.ex[:, a:b], T.ki[:, 0:b - a], T.MN[:, H + a:H + b], 0.0, Op.add, Op.max))
 
         def listed(a, b):
-            emit("v", [("lz", a // 16, b // 16)], [("ex", a, b), whole("cold")],
-                 lambda e: e.tensor_scalar(T.lz[:, a // 16:b // 16], T.ex[:, a + 15:b:16], T.cold[:, 0:1], 2.0 ** 20, Op.subtract, Op.mult))
+            emit("v", [("lz", a // 16, b // 16)], [("ex", a, b), whole("coli")],
+                 lambda e: e.tensor_scalar(T.lz[:, a // 16:b // 16], T.ex[:, a + 15:b:16], T.coli[:, 0:1], None, Op.subtract))
 
         def gather(qn, b, h):
-            a, e1 = HALVES[h]
+            a, e1 = PARTS[h]
             out, src = T.z[:, 4 * a + b:4 * e1:4], T["F%d" % b][:, 0:H + C].indirect(T.lz[:, a // 16:e1 // 16])
             outs, ins = [("z", 4 * a + b, 4 * a + b + 1)], [whole("F%d" % b), ("lz", a // 16, e1 // 16)]
             if qn == "v":
@@ -354,56 +394,59 @@ def rank_program(g, core, T, topo):
             else:
                 emit("s", outs, ins, lambda e: e.activation(out, src, Act.Copy))
 
-        for i in range(C // 64):
-            c = H + 64 * i
-            emit("v", [("MN", c, c + 64)], [("MN", 0, c), ("L3", 4 * i, 4 * i + 4), ("U2", D, D + C)],
-                 lambda e: e.tensor_tensor(T.MN[:, c:c + 64], T.MN[:, 0:c].indirect(T.L3[:, 4 * i:4 * i + 4]), T.U2[:, D + i:D + C:7], Op.max))
-            if i > 0:
-                collect(64 * i - 64, 64 * i)
-            if 64 * i - 64 == LO:
-                listed(0, LO)
-        collect(C - 64, C)
-        listed(LO, C)
-        for b in range(4):
-            gather("vvss"[b], b, 0)
-        if last:
-            quant("vq", "vs", "vt", 0, 128)
-        quant("zq", "zs", "z", LO, C)
-        for b in range(4):
-            gather("vvss"[b], b, 1)
-        quant("zq", "zs", "z", 0, LO)
-        for h in range(2):
-            for b in range(4):
-                product(4 * h + b, W, 128 * b, ("zq", "zs"), HALVES[h][0], HALVES[h][1], False, True)
-
         def finish(qn, h, b):
-            a, e1 = HALVES[h]
-            bank = 4 * h + b
+            a, e1 = PARTS[h]
+            bank = 4 - 4 * h + b
             copy(qn, T[new][:, 4 * a + b:4 * e1:4], (new, 4 * a + b, 4 * a + b + 1), T.ps[:, 512 * bank:512 * bank + e1 - a], psum(bank), 2.0 ** -6)
 
         q = ("q%d" % (t + 1), "s%d" % (t + 1))
-        for b in range(4):
-            finish("svsv"[b], 0, b)
-        quant(q[0], q[1], new, LO, C)
-        if last:
-            store("y", T.oc[:, 4 * LO:4 * C], T[q[0]][:, LO:C].bitcast(dt.uint8), (q[0], LO, C))
-        else:
-            send(t + 1)
-        product(0, V if last else U, 0, q, LO, C)
-        for b in range(4):
-            finish("svsv"[b], 1, b)
-        quant(q[0], q[1], new, 0, LO)
-        product(1, V if last else U, 0, q, 0, LO)
+        for step in ROUND.split():
+            k = step[0]
+            if k == "m":
+                block(int(step[1:]))
+                continue
+            if k == "c":
+                a, b = step[1:].split(":")
+                collect(64 * int(a), 64 * int(b))
+                continue
+            if k == "x" or k == "v":
+                if k == "v" and last:
+                    quant("vq", "vs", "vt", 0, 128)
+                elif k == "x" and not last:
+                    send(t + 1)
+                continue
+            h = "AB".index(step[1])
+            a, b = PARTS[h]
+            if k == "l":
+                listed(a, b)
+            elif k == "g":
+                gather(step[3], int(step[2]), h)
+            elif k == "z":
+                quant("zq", "zs", "z", a, b)
+            elif k == "w":
+                n = int(step[2])
+                product(4 - 4 * h + n, W, 128 * n, ("zq", "zs"), a, b, False, True)
+            elif k == "f":
+                finish(step[3], h, int(step[2]))
+            elif k == "q":
+                quant(q[0], q[1], new, a, b)
+                if last:
+                    store("y", T.oc[:, 4 * a:4 * b], T[q[0]][:, a:b].bitcast(dt.uint8), (q[0], a, b))
+            elif k == "u":
+                product(4 + h, V if last else U, 0, q, a, b)
+            elif k == "d" and last:
+                c = 2048 + 512 * h
+                copy(step[2], T.yt[:, a:b], ("yt", a, b), T.ps[:, c:c + b - a], psum(4 + h), 1.0)
+                store("sy"[h], T.y[:, a:b], T.yt[:, a:b], ("yt", a, b))
+            elif k == "d":
+                decide(h, step[2])
+            elif k == "p" and not last:
+                places(h)
 
-    copy("s", T.yt[:, LO:C], ("yt", LO, C), T.ps[:, 0:H], psum(0), 1.0)
-    store("s", T.y[:, LO:C], T.yt[:, LO:C], ("yt", LO, C))
-    copy("v", T.yt[:, 0:LO], ("yt", 0, LO), T.ps[:, 512:512 + LO], psum(1), 1.0)
-    copy("s", T.olt[:], whole("olt"), T.MN[:, H:H + C], ("MN", H, H + C), 2.0 ** 20, -float(H))
+    copy("s", T.olt[:], whole("olt"), T.MN[:, H:H + C], ("MN", H, H + C), 1.0, -float(H))
     store("s", T.ol[:], T.olt[0:128:16, :], whole("olt"))
-    store("y", T.oc[:, 0:4 * LO], T[q[0]][:, 0:LO].bitcast(dt.uint8), (q[0], 0, LO))
     for k in range(4):
         store("y" if k < 2 else "s", T.osc[4 * k:4 * k + 4, :], T[q[1]][32 * k:32 * k + 4, :], (q[1], 0, C))
-    store("y", T.y[:, 0:LO], T.yt[:, 0:LO], ("yt", 0, LO))
     for sem in SEMAPHORES:
         if total[sem]:
             g.wait_ge(T.sem[sem], total[sem])

from concourse.mybir import AluOpType as Op, ActivationFunctionType as Act, dt

F32, B16, I32, U16, U8, X4 = "float32", "bfloat16", "int32", "uint16", "uint8", "float8_e4m3fn_x4"
C, H, R = 448, 256, 3
LO = C - H
SPLIT = 192
PARTS = ((0, SPLIT), (SPLIT, C))
HEAD = ("oA2 oB2 U01 U02 oA1 U03 oA0 U1v U1s U11 oA3 U12 oB0 U13 U2s oB1 oB3 h0 h1 h2 U2v h3 U21 e1 U22 e0 U23 E0 E3 E1 E2 "
        "e2 e3")
ROUND = ("m0 m1 m2 m3 c0:3 lA m4 m5 m6 gA3s gA1s c3:6 gA2s c6:7 gA0v lB zA gB2v gB3s wA3 wA1 gB0s fA1s wA2 wA0 gB1v zB v "
         "fA2s wB3 wB1 fB3v wB0 fA0s fA3s wB2 fB1s qA fB0v uA fB2v qB x dAs pA uB dBv pB")
OWN = (6, 7, 4, 5)
LEVELS = (4, 16, 64)
RUN, D = C // 4, 16

SCRATCH = {
    "z": ("sbuf", [128, 4 * C], B16), "xt": ("sbuf", [128, 4 * C], B16),
    "zq": ("sbuf", [128, C], X4), "zs": ("sbuf", [128, C], U8),
    "wq": ("sbuf", [128, 512], X4), "wp": ("sbuf", [128, 512], U8),
    "ut": ("sbuf", [128, 512], B16), "vt": ("sbuf", [128, 512], B16),
    "ua": ("sbuf", [128, 128], X4), "uas": ("sbuf", [128, 128], U8),
    "uq": ("sbuf", [128, 128], X4), "us": ("sbuf", [128, 128], U8),
    "vq": ("sbuf", [128, 128], X4), "vs": ("sbuf", [128, 128], U8),
    "one": ("sbuf", [128, 516], B16), "et": ("sbuf", [128, 516], B16), "eq": ("sbuf", [128, 512], X4), "es": ("sbuf", [128, 512], U8),
    "MN": ("sbuf", [128, H + C], F32), "ff": ("sbuf", [128, C], F32),
    "ex": ("sbuf", [128, C], F32), "exs": ("sbuf", [128, 384], F32), "exn": ("sbuf", [128, C], F32),
    "ki": ("sbuf", [128, H], F32), "kt": ("sbuf", [128, RUN], I32), "kb": ("sbuf", [128, RUN], I32), "kd": ("sbuf", [128, RUN], F32),
    "p1": ("sbuf", [128, C], F32), "db": ("sbuf", [128, C], I32),
    "pa": ("sbuf", [128, 2], I32), "pm": ("sbuf", [128, 2], I32), "pm3": ("sbuf", [128, 2], I32), "pm4": ("sbuf", [128, 2], I32),
    "pf": ("sbuf", [128, 2], F32), "p3": ("sbuf", [128, 2], F32), "pe": ("sbuf", [128, 2], F32),
    "c1": ("sbuf", [128, 28], F32), "gn": ("sbuf", [128, 24], F32), "nn": ("sbuf", [128, 24], F32),
    "ul": ("sbuf", [128, 8], I32), "lu": ("sbuf", [128, 8], U16),
    "coli": ("sbuf", [128, 2], F32), "colm": ("sbuf", [128, 2], F32),
    "lc": ("sbuf", [128, 28], U16), "lz": ("sbuf", [128, 28], U16), "L3": ("sbuf", [128, 28], U16),
    "yt": ("sbuf", [128, C], F32), "olt": ("sbuf", [128, C], F32),
    "ps": ("psum", [128, 4096], F32),
}
for _i in range(3):
    SCRATCH["U%d" % _i] = ("sbuf", [128, D + C], F32)
    SCRATCH["X%d" % _i] = ("sbuf", [128, D + C], F32)
    SCRATCH["L%d" % _i] = ("sbuf", [128, 24], U16)
    for _n in ("ra", "tb", "td", "te", "cc"):
        SCRATCH["%s%d" % (_n, _i)] = ("sbuf", [128, 24], F32)
    SCRATCH["ti%d" % _i] = ("sbuf", [128, 24], I32)
    SCRATCH["hq%d" % _i] = ("sbuf", [128, H], X4)
    SCRATCH["hs%d" % _i] = ("sbuf", [128, H], U8)
for _i in range(4):
    SCRATCH["F%d" % _i] = ("sbuf", [128, H + C], B16)
    SCRATCH["q%d" % _i] = ("sbuf", [128, C], X4)
    SCRATCH["s%d" % _i] = ("sbuf", [128, C], U8)
for _i in range(1, R + 1):
    SCRATCH["t%d" % _i] = ("sbuf", [128, 4 * C], B16)

SEMAPHORES = ["cv", "cs", "ct", "cp", "sent", "arr0", "arr1", "arr2", "ldxa", "ldxb", "ldu", "ldw", "ldb", "ldv", "out"]


def rank_program(g, core, T, topo):
    rank = T.rank_of(core)
    if rank is None:
        return
    n_ranks = len(T.cores)
    queue = {"v": g.vector, "s": g.scalar, "t": g.tensor, "p": g, "y": g.sync}
    total = {s: 0 for s in SEMAPHORES}
    clock = {q: {} for q in queue}
    log = {}

    def know(q, tok):
        sem, n, snap = tok
        if clock[q].get(sem, 0) >= n:
            return
        queue[q].wait_ge(T.sem[sem], n)
        for s, m in snap.items():
            clock[q][s] = max(clock[q].get(s, 0), m)
        clock[q][sem] = n

    def depend(q, outs, ins):
        need = {}
        for acc, write in [(a, True) for a in outs] + [(a, False) for a in ins]:
            name, a, b = acc
            for (c, d, w, oq, tok) in log.get(name, []):
                if not (a < d and c < b):
                    continue
                if name == "ps":
                    if oq == q and (q == "t" or not (w or write)):
                        continue
                elif not (w or write):
                    continue
                old = need.get(tok[0])
                if old is None or old[1] < tok[1]:
                    need[tok[0]] = tok
        for tok in sorted(need.values(), key=lambda t: -len(t[2])):
            know(q, tok)

    def note(q, outs, ins, tok):
        for acc, write in [(a, True) for a in outs] + [(a, False) for a in ins]:
            name, a, b = acc
            old = log.setdefault(name, [])
            if write:
                old[:] = [e for e in old if not (a <= e[0] and e[1] <= b)]
            old.append((a, b, write, q, tok))

    def emit(q, outs, ins, call):
        depend(q, outs, ins)
        sem = "c" + q
        call(queue[q]).then_inc(T.sem[sem], 1)
        total[sem] += 1
        note(q, outs, ins, (sem, total[sem], dict(clock[q])))

    def load(q, out, acc, in_, sem, upto):
        queue[q].dma_start(out, in_).then_inc(T.sem[sem], 16)
        total[sem] += 16
        note(q, [acc], [], (sem, upto, dict(clock[q])))

    def store(q, out, in_, acc):
        depend(q, [], [acc])
        queue[q].dma_start(out, in_).then_inc(T.sem["out"], 16)
        total["out"] += 16

    def copy(q, out, oacc, in_, iacc, scale, bias=0.0):
        if q == "v":
            emit("v", [oacc], [iacc], lambda e: e.tensor_scalar(out, in_, scale, None, Op.mult))
        else:
            emit("s", [oacc], [iacc], lambda e: e.activation(out, in_, Act.Copy, bias=bias, scale=scale))

    def whole(name):
        return (name, 0, SCRATCH[name][1][1])

    def affine(out, in_, scale, bias=0.0):
        copy("s", T[out][:], whole(out), T[in_][:], whole(in_), scale, bias)

    def plus(out, in_, col):
        emit("s", [whole(out)], [whole(in_), whole(col)], lambda e: e.activation(T[out][:], T[in_][:], Act.Identity, bias=T[col][:, 0:1]))

    def small(out, in_, s1, s2, *ops):
        a1 = T[s1][:, 0:1] if isinstance(s1, str) else s1
        ins = [whole(in_)] + ([whole(s1)] if isinstance(s1, str) else [])
        emit("v", [whole(out)], ins, lambda e: e.tensor_scalar(T[out][:], T[in_][:], a1, s2, *ops))

    def both(out, a, b, op):
        emit("v", [whole(out)], [whole(a), whole(b)], lambda e: e.tensor_tensor(T[out][:], T[a][:], T[b][:], op))

    def cast(out, in_):
        emit("v", [whole(out)], [whole(in_)], lambda e: e.tensor_copy(T[out][:], T[in_][:]))

    def quant(qn, sn, tn, a, b):
        emit("v", [(qn, a, b), (sn, a, b)], [(tn, 4 * a, 4 * b)],
             lambda e: e.quantize_mx(T[qn][:, a:b], T[sn][:, a:b], T[tn][:, 4 * a:4 * b]))

    def psum(bank):
        return ("ps", 512 * bank, 512 * bank + 512)

    def product(bank, st, c0, mv, a, b, start=True, stop=True):
        n = b - a
        emit("t", [psum(bank)], [(st[0], c0, c0 + 128), (st[1], c0, c0 + 128), (mv[0], a, b), (mv[1], a, b)],
             lambda e: e.matmul_mx(T.ps[:, 512 * bank:512 * bank + n], T[st[0]][:, c0:c0 + 128], T[st[1]][:, c0:c0 + 128],
                                   T[mv[0]][:, a:b], T[mv[1]][:, a:b], start, stop))

    def unpack(b, c, d, bank):
        n = d - c
        copy("s", T["F%d" % b][:, c:d], ("F%d" % b, c, d), T.ps[:, 512 * bank:512 * bank + n], psum(bank), 2.0 ** -6)

    def iota(name, pattern, base, mult, b=None):
        b = b or SCRATCH[name][1][1]
        if SCRATCH[name][2] == I32:
            emit("p", [(name, 0, b)], [], lambda e: e.iota(T[name][:, 0:b], pattern, base, mult))
        else:
            emit("p", [(name, 0, b)], [], lambda e: e.iota(T[name][:, 0:b], pattern, base, mult, allow_small_or_imprecise_dtypes=True))

    E, W, U, V = ("eq", "es"), ("wq", "wp"), ("uq", "us"), ("vq", "vs")

    for i in range(16):
        load("ys"[i % 2], T.db[i:128:16, :], ("db", 0, C), T.dist[:], "ldb", 256)
    load("y", T.xt[:, 0:4 * SPLIT], ("xt", 0, 4 * SPLIT), T.x[:, 0:4 * SPLIT], "ldxa", 16)
    load("s", T.ut[:], ("ut", 0, 512), T.u[:], "ldu", 16)
    load("s", T.xt[:, 4 * SPLIT:4 * C], ("xt", 4 * SPLIT, 4 * C), T.x[:, 4 * SPLIT:4 * C], "ldxb", 16)
    load("y", T.wq[:].bitcast(dt.uint8), ("wq", 0, 512), T.wc[:], "ldw", 32)
    load("y", T.wp[:], ("wp", 0, 512), T.ws[:], "ldw", 32)
    load("y", T.vt[:], ("vt", 0, 512), T.v[:], "ldv", 16)

    iota("pa", [[0, 2]], 0, 1)
    iota("c1", [[28, 4], [4, 7]], 0, 0)
    iota("gn", [[0, 3], [16, 8]], 0, 0)
    iota("kt", [[0, 7], [1, 16]], 128, -1)
    iota("ul", [[16, 8]], 0, 0)
    iota("p1", [[1, 4], [4, RUN]], H, 0)
    iota("one", [[0, 516]], 64, 0)
    emit("p", [whole("et")], [whole("one")], lambda e: e.affine_select(T.et[:], T.one[:], [[-1, 516]], Op.is_equal, 0.0, 3, 4))
    iota("MN", [[1, H]], 0, 0, H)
    small("pm3", "pa", 3, None, Op.bitwise_and)
    small("pm4", "pa", 15, 2, Op.bitwise_and, Op.arith_shift_right)
    small("pm", "pa", 15, None, Op.bitwise_and)
    small("p3", "pm3", float(RUN), None, Op.mult)
    cast("pf", "pm")
    both("pe", "p3", "pm4", Op.add)
    small("lc", "c1", "pe", None, Op.add)
    small("kb", "kt", 15, None, Op.bitwise_and)
    small("kd", "kb", 1.0, 1.0 - 2.0 ** -10, Op.min, Op.subtract)
    cast("lu", "ul")
    if rank == 0:
        for b in range(4):
            emit("v", [("F%d" % b, 0, H)], [], lambda e: e.memset(T["F%d" % b][:, 0:H], 0.0))

    def nothing(name, value):
        copy("s", T[name][:, 0:D], (name, 0, D), T.c1[:, 0:D], whole("c1"), 0.0, value)

    def keep(a):
        n = min(RUN, H - a)
        copy("s", T.ki[:, a:a + n], ("ki", a, a + n), T.kd[:, 0:n], whole("kd"), 2.0 ** 20)

    COUNTS = ((0, RUN), (1, RUN // 4), (2, RUN // 16))
    plus("nn", "gn", "pf")
    affine("colm", "pf", 1024.0, -15360.0)
    keep(0)
    copy("s", T.exs[:, 127:384:128], whole("exs"), T.c1[:, 0:3], whole("c1"), 0.0)
    for i, k in COUNTS:
        affine("td%d" % i, "nn", (C - 1.0) / k, (k * H - D - 0.25) / k)
        plus("te%d" % i if i else "cc0", "td%d" % i, "colm")
    nothing("X0", -30000.0)
    for i, k in COUNTS[1:]:
        small("ti%d" % i, "nn", -(k - 1) / 2.0, 1.0 / k, Op.add, Op.mult)
        small("tb%d" % i, "ti%d" % i, -(C - 1.0), None, Op.mult)
    for i, k in COUNTS[1:]:
        both("cc%d" % i, "te%d" % i, "tb%d" % i, Op.add)

    def send(t):
        if rank + 1 == n_ranks:
            return
        dst = T.cores[rank + 1]
        rid, pid = topo.addr(dst)[:2]
        depend("p", [], [("q%d" % t, LO, C), ("s%d" % t, LO, C)])
        for out, in_ in ((T["hq%d" % t][:].bitcast(dt.uint8), T["q%d" % t][:, LO:C].bitcast(dt.uint8)), (T["hs%d" % t][:], T["s%d" % t][:, LO:C])):
            g.remote_dma(out, in_, T.sem["arr%d" % t], T.sem.sent, pid, rid, topo.mask(core, dst))
            total["sent"] += len(topo.engines(core, dst))

    def arrives(t):
        n = len(topo.engines(T.cores[rank - 1], core))
        for name in ("hq%d" % t, "hs%d" % t):
            log[name] = [(0, H, True, "far", ("arr%d" % t, 2 * n, {}))]

    def row(i):
        for s in range(1, 4):
            a, c = D + RUN * s, 128 * s - 128
            src = T.X0[:, a:a + RUN] if i is None else T["X%d" % i][:, D + s:D + C:4]
            emit("v", [("exs", c, c + RUN)], [("ki", 0, RUN), ("X%d" % (i or 0), D, D + C)],
                 lambda e: e.tensor_tensor_scan(T.exs[:, c:c + RUN], T.ki[:, 0:RUN], src, 0.0, Op.add, Op.max))

    def listing(i, k, between=None):
        emit("v", [whole("ra%d" % i)], [whole("exs"), whole("cc%d" % i)],
             lambda e: e.tensor_tensor(T["ra%d" % i][:], T.exs[:, 15:384:16], T["cc%d" % i][:], Op.add))
        if between:
            between()
        small("L%d" % i, "ra%d" % i, -float(k), None, Op.mult)

    def merge(kind, i, s):
        dst, src = "%s%d" % (kind, i), "%s%d" % (kind, i - 1)
        a = D + RUN * s
        out, oacc = T[dst][:, a:a + RUN], (dst, a, a + RUN)
        if i == 0:
            old, iacc = out, oacc
        else:
            old, iacc = T[src][:, D + s:D + C:4], (src, D, D + C)
        emit("v", [oacc], [(dst, 0, a), whole("L%d" % i), iacc],
             lambda e: e.tensor_tensor(out, T[dst][:, 0:a].indirect(T["L%d" % i][:, 8 * s - 8:8 * s - 1]), old, Op.max))

    def first(kind, i, qn, r0, r1):
        dst, src = "%s%d" % (kind, i), "%s%d" % (kind, i - 1)
        a, b, c, d = D + RUN // 4 * r0, D + RUN // 4 * r1, D + RUN * r0, D + RUN * r1
        copy(qn, T[dst][:, a:b], (dst, a, b), T[src][:, c:d:4], (src, c, d), 1.0)

    def decide(h, qn):
        a, b = PARTS[h]
        in_, bank = T.ps[:, 2048 + 512 * h:2048 + 512 * h + b - a], psum(4 + h)
        if qn == "v":
            emit("v", [("ff", a, b)], [bank], lambda e: e.tensor_scalar(T.ff[:, a:b], in_, 0.0, None, Op.is_ge))
        else:
            emit("s", [("ff", a, b)], [bank], lambda e: e.activation(T.ff[:, a:b], in_, Act.Sign, bias=2.0 ** -100))

    def places(h):
        a, b = PARTS[h]
        for s in range(4):
            c, d = RUN * s + a // 4, RUN * s + b // 4
            emit("v", [("U0", D + c, D + d)], [("ff", a, b), ("p1", c, d)],
                 lambda e: e.tensor_tensor_scan(T.U0[:, D + c:D + d], T.p1[:, c:d], T.ff[:, a + s:b:4], 0.0, Op.max, Op.mult))

    emit("v", [("X0", D, D + C)], [whole("db"), whole("lc"), whole("p1")],
         lambda e: e.tensor_tensor(T.X0[:, D:D + C], T.db[:].indirect(T.lc[:]), T.p1[:], Op.subtract))
    row(None)
    listing(0, RUN)
    quant("ua", "uas", "ut", 0, 128)
    emit("s", [whole("us")], [whole("uas"), whole("lu")], lambda e: e.activation(T.us[:], T.uas[:].indirect(T.lu[:]), Act.Copy))
    quant("q0", "s0", "xt", 0, SPLIT)
    nothing("U0", -1.0)
    keep(RUN)
    for i in (1, 2):
        nothing("X%d" % i, -30000.0)
        nothing("U%d" % i, -1.0)
    affine("coli", "pf", -1024.0, 15360.0)
    emit("v", [whole("uq")], [whole("ua"), whole("lu")],
         lambda e: e.tensor_copy(T.uq[:].bitcast(dt.uint32), T.ua[:].bitcast(dt.uint32).indirect(T.lu[:])))
    keep(2 * RUN)
    product(4, U, 0, ("q0", "s0"), 0, SPLIT)
    decide(0, "s")
    quant("q0", "s0", "xt", SPLIT, C)
    send(0)
    product(5, U, 0, ("q0", "s0"), SPLIT, C)
    merge("X", 0, 1)
    for b in range(4):
        c = 128 * b
        emit("v", [("eq", c, c + 128), ("es", c, c + 128)], [whole("et")],
             lambda e: e.quantize_mx(T.eq[:, c:c + 128], T.es[:, c:c + 128], T.et[:, 3 - b:515 - b]))
    places(0)
    decide(1, "v")
    places(1)

    for t in range(R):
        q = ("q%d" % t, "s%d" % t)
        land = ("hq%d" % t, "hs%d" % t)
        new = "t%d" % (t + 1)
        last = t + 1 == R
        if rank > 0:
            arrives(t)

        def head(step):
            k, h, b = step[0], "AB".find(step[1]), step[2] if step[0] in "oU" else step[1]
            if k == "U":
                if b == "s":
                    first("U", int(step[1]), "s", 0, 3)
                elif b == "v":
                    first("U", int(step[1]), "v", 3, 4)
                else:
                    merge("U", int(step[1]), int(b))
                return
            b = int(b)
            if k == "o":
                a, e1 = PARTS[h]
                bank = b if h else OWN[b]
                product(bank, E, 128 * b, q, a, e1)
                unpack(b, H + a, H + e1, bank)
            elif k == "h" and rank > 0:
                product(4 + b, E, 128 * b, land, 0, H)
                unpack(b, 0, H, 4 + b)
            elif k == "e":
                product(4 + b, E, 128 * b, q, 0, SPLIT, True, False)
            elif k == "E":
                product(b, E, 128 * b, q, SPLIT, C, True, False)

        if t == 0:
            for i in range(3):
                if i > 0:
                    first("X", i, "s", 0, 4)
                    first("U", i, "s", 0, 4)
                for s in range(1, 4):
                    if (i, s) != (0, 1):
                        merge("X", i, s)
                    if s < 3 or i == 2:
                        merge("U", i, s)
                if i < 2:
                    row(i)
                    listing(i + 1, RUN // LEVELS[i], lambda: merge("U", i, 3))
                if i > 0:
                    for b in range(4):
                        head("o" + " AB"[i] + str(b))
            for s in range(7):
                emit("v", [("exn", 64 * s, 64 * s + 64)], [("ki", 0, 64), ("X2", D, D + C)],
                     lambda e: e.tensor_tensor_scan(T.exn[:, 64 * s:64 * s + 64], T.ki[:, 0:64], T.X2[:, D + s:D + C:7], 0.0, Op.add, Op.max))
            emit("v", [whole("L3")], [whole("exn"), whole("coli")],
                 lambda e: e.tensor_scalar(T.L3[:], T.exn[:, 15:C:16], T.coli[:, 0:1], -1.0, Op.subtract, Op.mult))
            for k in "heE":
                for b in range(4):
                    head(k + str(b))
        else:
            for step in HEAD.split():
                head(step)

        def block(i):
            c = H + 64 * i
            emit("v", [("MN", c, c + 64)], [("MN", 0, c), ("L3", 4 * i, 4 * i + 4), ("U2", D, D + C)],
                 lambda e: e.tensor_tensor(T.MN[:, c:c + 64], T.MN[:, 0:c].indirect(T.L3[:, 4 * i:4 * i + 4]), T.U2[:, D + i:D + C:7], Op.max))

        def collect(a, b):
            emit("v", [("ex", a, b)], [("ki", 0, b - a), ("MN", H + a, H + b)],
                 lambda e: e.tensor_tensor_scan(T.ex[:, a:b], T.ki[:, 0:b - a], T.MN[:, H + a:H + b], 0.0, Op.add, Op.max))

        def listed(a, b):
            emit("v", [("lz", a // 16, b // 16)], [("ex", a, b), whole("coli")],
                 lambda e: e.tensor_scalar(T.lz[:, a // 16:b // 16], T.ex[:, a + 15:b:16], T.coli[:, 0:1], None, Op.subtract))

        def gather(qn, b, h):
            a, e1 = PARTS[h]
            out, src = T.z[:, 4 * a + b:4 * e1:4], T["F%d" % b][:, 0:H + C].indirect(T.lz[:, a // 16:e1 // 16])
            outs, ins = [("z", 4 * a + b, 4 * a + b + 1)], [whole("F%d" % b), ("lz", a // 16, e1 // 16)]
            if qn == "v":
                emit("v", outs, ins, lambda e: e.tensor_copy(out, src))
            else:
                emit("s", outs, ins, lambda e: e.activation(out, src, Act.Copy))

        def finish(qn, h, b):
            a, e1 = PARTS[h]
            bank = 4 - 4 * h + b
            copy(qn, T[new][:, 4 * a + b:4 * e1:4], (new, 4 * a + b, 4 * a + b + 1), T.ps[:, 512 * bank:512 * bank + e1 - a], psum(bank), 2.0 ** -6)

        q = ("q%d" % (t + 1), "s%d" % (t + 1))
        for step in ROUND.split():
            k = step[0]
            if k == "m":
                block(int(step[1:]))
                continue
            if k == "c":
                a, b = step[1:].split(":")
                collect(64 * int(a), 64 * int(b))
                continue
            if k == "x" or k == "v":
                if k == "v" and last:
                    quant("vq", "vs", "vt", 0, 128)
                elif k == "x" and not last:
                    send(t + 1)
                continue
            h = "AB".index(step[1])
            a, b = PARTS[h]
            if k == "l":
                listed(a, b)
            elif k == "g":
                gather(step[3], int(step[2]), h)
            elif k == "z":
                quant("zq", "zs", "z", a, b)
            elif k == "w":
                n = int(step[2])
                product(4 - 4 * h + n, W, 128 * n, ("zq", "zs"), a, b, False, True)
            elif k == "f":
                finish(step[3], h, int(step[2]))
            elif k == "q":
                quant(q[0], q[1], new, a, b)
                if last:
                    store("y", T.oc[:, 4 * a:4 * b], T[q[0]][:, a:b].bitcast(dt.uint8), (q[0], a, b))
            elif k == "u":
                product(4 + h, V if last else U, 0, q, a, b)
            elif k == "d" and last:
                c = 2048 + 512 * h
                copy(step[2], T.yt[:, a:b], ("yt", a, b), T.ps[:, c:c + b - a], psum(4 + h), 1.0)
                store("sy"[h], T.y[:, a:b], T.yt[:, a:b], ("yt", a, b))
            elif k == "d":
                decide(h, step[2])
            elif k == "p" and not last:
                places(h)

    copy("s", T.olt[:], whole("olt"), T.MN[:, H:H + C], ("MN", H, H + C), 1.0, -float(H))
    store("s", T.ol[:], T.olt[0:128:16, :], whole("olt"))
    for k in range(4):
        store("y" if k < 2 else "s", T.osc[4 * k:4 * k + 4, :], T[q[1]][32 * k:32 * k + 4, :], (q[1], 0, C))
    for sem in SEMAPHORES:
        if total[sem]:
            g.wait_ge(T.sem[sem], total[sem])
